import numpy as np
import ml_dtypes


def mxq(x, axis, fmt="e4m3"):
    dtype, down = {"e4m3": (ml_dtypes.float8_e4m3fn, 7), "e5m2": (ml_dtypes.float8_e5m2, 14)}[fmt]
    v = np.moveaxis(np.asarray(x, np.float32).astype(ml_dtypes.bfloat16).astype(np.float64), axis, -1)
    blocks = v.reshape(v.shape[:-1] + (-1, 32))
    amax = np.abs(blocks).max(-1, keepdims=True)
    byte = np.maximum(np.where(amax > 0, np.frexp(amax)[1] - 1 + 127, 0) - down, 1)
    scale = np.exp2(byte - 127.0)
    codes = (blocks / scale).astype(np.float32).astype(dtype).astype(np.float64)
    return np.moveaxis((codes * scale).reshape(v.shape), -1, axis)


WIDE = False


def mx_kscale(k):
    if not WIDE:
        return np.ones(k)
    levels = np.array([10, -10, 5, -5, 0])
    if k % 512:
        return np.exp2(np.random.permutation(np.resize(levels, k // 32))).repeat(32)
    a = np.empty((k // 512, 16))
    for p in range(k // 512):
        a[p, :8] = np.random.permutation(np.resize(levels, 8))
        for g in range(8):
            far = levels[np.abs(levels - a[p, g]) >= 10]
            a[p, g + 8] = far[np.random.randint(len(far))]
    return np.exp2(a.ravel()).repeat(32)


BF16 = ml_dtypes.bfloat16


def bf(x):
    return np.asarray(x, np.float32).astype(BF16)


def f64(x):
    return np.asarray(x).astype(np.float64)


E2M1 = np.array([0.0, 0.5, 1.0, 1.5, 2.0, 3.0, 4.0, 6.0, -0.0, -0.5, -1.0, -1.5, -2.0, -3.0, -4.0, -6.0])


def pack_weight(w, fmt):
    k, n = w.shape
    w = f64(bf(w)).reshape(k // 32, 32, n)
    amax = np.abs(w).max(1)
    if fmt == "e4m3":
        byte = np.frexp(amax)[1] - 1 + 127 - 7
    else:
        mant, ex = np.frexp(amax / 6.0)
        byte = np.where(mant > 0.5, ex, ex - 1) + 127
    byte = np.clip(np.where(amax > 0, byte, 1), 1, 254)
    scaled = (w * np.exp2(127.0 - byte)[:, None, :]).reshape(k, n).astype(np.float32)
    by_word = np.ascontiguousarray(scaled.reshape(k // 512, 128, 4, n).transpose(0, 1, 3, 2))
    if fmt == "e4m3":
        words = by_word.astype(ml_dtypes.float8_e4m3fn).view(np.uint8)
    else:
        c = by_word.astype(ml_dtypes.float4_e2m1fn).view(np.uint8) & 0xF
        words = c[..., 0::2] | (c[..., 1::2] << 4)
    return np.ascontiguousarray(words), np.ascontiguousarray(byte.astype(np.uint8).reshape(k // 512, 16, n))


def unpack_weight(words, scales, fmt):
    g, p, n, _ = words.shape
    if fmt == "e4m3":
        vals = np.ascontiguousarray(words).view(ml_dtypes.float8_e4m3fn).astype(np.float64)
    else:
        nib = np.empty((g, p, n, 4), np.uint8)
        nib[..., 0::2] = words & 0xF
        nib[..., 1::2] = words >> 4
        vals = E2M1[nib]
    vals = vals * np.repeat(np.exp2(scales.astype(np.float64) - 127.0), 8, axis=1)[..., None]
    return vals.transpose(0, 1, 3, 2).reshape(g * 512, n)

def planes(Y):
    n, m = Y.shape
    b = f64(bf(Y)).reshape(n // 32, 32, m)
    amax = np.abs(b).max(1)
    byte = np.clip(np.where(amax > 0, np.frexp(amax)[1] - 1 + 127 - 7, 1), 1, 254)
    codes = (b * np.exp2(127.0 - byte)[:, None, :]).reshape(n, m).astype(np.float32).astype(ml_dtypes.float8_e4m3fn).view(np.uint8)
    words = codes.reshape(n // 512, 128, 4, m).transpose(0, 1, 3, 2)
    return np.ascontiguousarray(words), np.ascontiguousarray(byte.astype(np.uint8).reshape(n // 512, 16, m))


T, B, D, N = 8, 128, 1024, 1024


def sigmoid(v):
    return 1.0 / (1.0 + np.exp(-v))


def softplus(v):
    return np.log(1.0 + np.exp(v))


def linear_recurrence(a, u):
    h = u[0]
    states = [h]
    for t in range(1, u.shape[0]):
        h = a[t] * h + u[t]
        states.append(h)
    return np.stack(states, axis=0)


def setup_inputs():
    s, t = mx_kscale(D), mx_kscale(D)
    x = bf(np.random.standard_normal((T, B, D)) * s)
    wr_words, wr_scales = pack_weight(np.random.standard_normal((D, D)) / np.sqrt(D) / s[:, None], "e4m3")
    wi_words, wi_scales = pack_weight(np.random.standard_normal((D, D)) / np.sqrt(D) / s[:, None], "e4m3")
    lam = bf(np.random.uniform(-3.0, -1.0, D))
    gain = bf((1.0 + 0.1 * np.random.standard_normal(D)) * t / s)
    wo_words, wo_scales = pack_weight(np.random.standard_normal((D, N)) / np.sqrt(D) / t[:, None], "e4m3")
    return {"x": x,
            "wr_words": wr_words, "wr_scales": wr_scales,
            "wi_words": wi_words, "wi_scales": wi_scales,
            "lam": lam,
            "gain": gain,
            "wo_words": wo_words, "wo_scales": wo_scales}


def core(x, wr_words, wr_scales, wi_words, wi_scales, lam, gain, wo_words, wo_scales):
    x = f64(x)
    xq = mxq(x, 2, "e4m3")
    r = sigmoid(xq @ unpack_weight(wr_words, wr_scales, "e4m3"))
    i = sigmoid(xq @ unpack_weight(wi_words, wi_scales, "e4m3"))
    a = np.exp(-8.0 * softplus(f64(lam)) * r)
    u = np.sqrt(1.0 - a * a) * (i * x)
    h = linear_recurrence(a, u)
    return mxq(h * f64(gain), 2, "e4m3") @ unpack_weight(wo_words, wo_scales, "e4m3")


def reference(x, wr_words, wr_scales, wi_words, wi_scales, lam, gain, wo_words, wo_scales):
    R_out = core(x, wr_words, wr_scales, wi_words, wi_scales, lam, gain, wo_words, wo_scales)
    words, scales = planes(np.moveaxis(R_out, 2, 0).reshape(1024, -1))
    return R_out, words, scales

@@ -1,0 +1,380 @@
+from contextlib import ExitStack
+
+import concourse.mybir as mybir
+from concourse.masks import make_identity
+
+T, B, D, N = 8, 128, 1024, 1024
+FLOPS = 3 * 2 * T * B * D * N
+
+F32 = mybir.dt.float32
+BF16 = mybir.dt.bfloat16
+I32 = mybir.dt.int32
+U8 = mybir.dt.uint8
+FP8X4 = mybir.dt.float8_e4m3fn_x4
+ACT = mybir.ActivationFunctionType
+ALU = mybir.AluOpType
+
+P = 128
+G = 2
+PACK = 4
+GC = 512
+CHUNKS = ((0, 4), (4, 4))
+SQ_ACT = ((0, 0), (0, 1))
+ROOTAT = (0, 0)
+QOAT = (1, 3, 5, 7, 10, 14)
+XE = "vavavvvv"
+OE_ROW = "aaaaaaaa"
+OE_COL = "aaaaaaaa"
+XLEAD = 1
+OUTLAG = 1
+
+
+def tile_rglrueightstepwithoutputprojection_x2_kernel(
+    tc, x, wr_words, wr_scales, wi_words, wi_scales, lam, gain, wo_words, wo_scales, out_0, out_1, out_2
+):
+    nc = tc.nc
+    with ExitStack() as ctx:
+        keep = ctx.enter_context(tc.tile_pool(name="keep", bufs=1))
+        pool = ctx.enter_context(tc.tile_pool(name="pool", bufs=2))
+        ps1 = ctx.enter_context(tc.psum_pool(name="ps1", bufs=4))
+        ps2 = ctx.enter_context(tc.psum_pool(name="ps2", bufs=4))
+        ctx.enter_context(tc.manual_schedule())
+
+        sraw_a = keep.tile([P, D], U8, name="sraw_a", align_bytes=64)
+        sraw_b = keep.tile([P, D], U8, name="sraw_b", align_bytes=64)
+        splane_a = keep.tile([P, D], U8, name="splane_a", align_bytes=64)
+        splane_b = keep.tile([P, D], U8, name="splane_b", align_bytes=64)
+        wp = {w: keep.tile([P, G, D], I32, name="wp_" + w, align_bytes=64) for w in ("r", "i", "o")}
+        plane = {("r", 0): (splane_a, 0), ("r", 1): (splane_a, 4), ("i", 0): (splane_a, 8), ("i", 1): (splane_a, 12),
+                 ("o", 0): (splane_b, 0), ("o", 1): (splane_b, 4)}
+        words = {"r": wr_words, "i": wi_words, "o": wo_words}
+        scales = {"r": wr_scales, "i": wi_scales, "o": wo_scales}
+
+        nc.vector.memset(sraw_a[:].bitcast(I32), 0)
+        nc.vector.memset(sraw_b[:].bitcast(I32), 0)
+
+        lam_sb = keep.tile([P, G, PACK], BF16, name="lam_sb")
+        gain_sb = keep.tile([P, G, PACK], BF16, name="gain_sb")
+        nc.scalar.dma_start(out=lam_sb[:], in_=lam.rearrange("(g p j) -> p g j", g=G, j=PACK))
+        nc.scalar.dma_start(out=gain_sb[:], in_=gain.rearrange("(g p j) -> p g j", g=G, j=PACK))
+        ident = keep.tile([P, P], F32, name="ident")
+        make_identity(nc, ident[:])
+
+        def load_scales(w, dst, row, queue):
+            for q in range(4):
+                queue.dma_start(
+                    out=dst[32 * q + row : 32 * q + row + 8, :].bitcast(I32),
+                    in_=scales[w][:, 4 * q : 4 * q + 4, :].bitcast(I32),
+                )
+
+        xraw = {}
+
+        def load_x(t):
+            xraw[t] = pool.tile([P, D], BF16, name="xraw", bufs=4)
+            nc.sync.dma_start(out=xraw[t][:], in_=x[t])
+
+        wraw = {}
+
+        def load_w(w, h):
+            wraw[w, h] = pool.tile([P, G, GC], I32, name="wraw", bufs=4)
+            nc.sync.dma_start(
+                out=wraw[w, h][:],
+                in_=words[w].rearrange("g p n t -> p g (n t)").bitcast(I32)[:, :, h * GC : (h + 1) * GC],
+            )
+
+        def permute_w(w, h):
+            nc.vector.tensor_copy(
+                out=wp[w][:, :, h * GC : (h + 1) * GC].rearrange("p k (j m) -> p k j m", j=PACK),
+                in_=wraw[w, h][:].rearrange("p k (m j) -> p k j m", j=PACK),
+            )
+
+        def permute_s(dst, src):
+            nc.vector.tensor_copy(
+                out=dst[:].rearrange("p (h j m) -> p h j m", h=G, j=PACK),
+                in_=src[:].rearrange("p (h m j) -> p h j m", h=G, j=PACK),
+            )
+
+        l1 = keep.tile([P, G * PACK], F32, name="l1")
+        l2 = keep.tile([P, G * PACK], F32, name="l2")
+        gain_f = keep.tile([P, G * PACK], F32, name="gain_f")
+
+        lam2 = lam_sb[:].rearrange("p g j -> p (g j)")
+        mag = keep.tile([P, G * PACK], F32, name="mag")
+        pos = keep.tile([P, G * PACK], F32, name="pos")
+
+        def softplus_act():
+            nc.scalar.activation(out=mag[:], in_=lam2, func=ACT.Abs)
+            nc.scalar.activation(out=mag[:], in_=mag[:], func=ACT.Exp, scale=-1.0)
+            nc.scalar.activation(out=mag[:], in_=mag[:], func=ACT.Ln, bias=1.0)
+
+        def softplus_vec():
+            nc.vector.tensor_copy(out=gain_f[:], in_=gain_sb[:].rearrange("p g j -> p (g j)"))
+            nc.vector.tensor_scalar_max(pos[:], lam2, 0.0)
+            nc.vector.tensor_tensor(out=pos[:], in0=pos[:], in1=mag[:], op=ALU.add)
+            nc.vector.tensor_scalar_mul(l1[:], pos[:], -4.0)
+            nc.vector.tensor_scalar_mul(l2[:], pos[:], -8.0)
+
+        home = {}
+        for c, (t0, nt) in enumerate(CHUNKS):
+            for k in range(nt):
+                home[t0 + k] = (c, slice(k * B, (k + 1) * B))
+
+        xt4, xq, xs = {}, {}, {}
+
+        def turn_x(t):
+            c, cols = home[t]
+            t0, nt = CHUNKS[c]
+            if t == t0:
+                xt4[c] = pool.tile([P, G, nt * B, 2], F32, name="xt4", align_bytes=64)
+            bank = ps2.tile([P, G, 2, B], F32, name="bank2")
+            w32 = xraw[t][:].bitcast(F32)
+            for g in range(G):
+                for u in range(2):
+                    nc.tensor.transpose(bank[:, g, u, :], w32[:, 256 * g + u : 256 * (g + 1) : 2], ident[:])
+            copy_out(XE[t], xt4[c][:, :, cols, :], bank[:].rearrange("p g u b -> p g b u"))
+
+        def xt_bf16(c, g):
+            return xt4[c][:, g, :, :].rearrange("p n u -> p (n u)").bitcast(BF16)
+
+        def quantize_x(c, g, part, parts):
+            t0, nt = CHUNKS[c]
+            if g == 0 and part == 0:
+                xq[c] = pool.tile([P, G, nt * B], I32, name="xq", align_bytes=64)
+                xs[c] = pool.tile([P, G, nt * B], U8, name="xs", align_bytes=64)
+            w = nt * B // parts
+            cols = slice(part * w, (part + 1) * w)
+            nc.vector.quantize_mx(
+                out=xq[c][:, g, cols].bitcast(FP8X4), scales=xs[c][:, g, cols],
+                in_=xt_bf16(c, g)[:, part * w * PACK : (part + 1) * w * PACK])
+
+        a, u, v, bank_r, bank_i = {}, {}, {}, {}, {}
+
+        def slots(c):
+            w = 4 // CHUNKS[c][1]
+            return [(g, j0, w) for g in range(G) for j0 in range(0, PACK, w)]
+
+        def gate_matmul(c, g, j0, w):
+            n = CHUNKS[c][1] * B
+            for name, banks in (("r", bank_r), ("i", bank_i)):
+                bank = ps1.tile([P, 512], F32, name="bank1")
+                banks[c, g, j0] = bank
+                for j in range(w):
+                    col = g * GC + (j0 + j) * P
+                    for k in range(G):
+                        sp, row = plane[name, k]
+                        nc.tensor.matmul_mx(
+                            out=bank[:, j * n : (j + 1) * n],
+                            lhsT=wp[name][:, k, col : col + P].bitcast(FP8X4),
+                            lhsT_scale=sp[row:P, col : col + P],
+                            rhs=xq[c][:, k, :].bitcast(FP8X4),
+                            rhs_scale=xs[c][:, k, :],
+                            start=(k == 0),
+                            stop=(k == G - 1),
+                        )
+
+        def flat(t_, j0, w):
+            return t_[:, j0 : j0 + w, :].rearrange("p j n -> p (j n)")
+
+        def gate_act(c, g, j0, w):
+            n = CHUNKS[c][1] * B
+            if g == 0 and j0 == 0:
+                a[c] = pool.tile([P, G, PACK, n], F32, name="a")
+                u[c] = pool.tile([P, G, PACK, n], F32, name="u")
+                v[c] = pool.tile([P, G, PACK, n], F32, name="v")
+            nc.scalar.activation(out=flat(a[c][:, g], j0, w), in_=bank_r[c, g, j0][:], func=ACT.Tanh, scale=0.5)
+            nc.scalar.activation(out=flat(u[c][:, g], j0, w), in_=bank_i[c, g, j0][:], func=ACT.Tanh, scale=0.5)
+            for j in range(j0, j0 + w):
+                col = slice(g * PACK + j, g * PACK + j + 1)
+                if SQ_ACT[c][g]:
+                    nc.scalar.activation(out=v[c][:, g, j, :], in_=a[c][:, g, j, :], func=ACT.Exp,
+                                         scale=l2[:, col], bias=l2[:, col])
+                nc.scalar.activation(out=a[c][:, g, j, :], in_=a[c][:, g, j, :], func=ACT.Exp,
+                                     scale=l1[:, col], bias=l1[:, col])
+
+        def gate_vec(c, g, j0, w):
+            xb = xt_bf16(c, g).rearrange("p (n j) -> p j n", j=PACK)
+            ug = u[c][:, g, j0 : j0 + w, :]
+            nc.vector.scalar_tensor_tensor(out=ug, in0=ug, scalar=1.0, in1=xb[:, j0 : j0 + w, :], op0=ALU.add, op1=ALU.mult)
+            if not SQ_ACT[c][g]:
+                ag = flat(a[c][:, g], j0, w)
+                nc.vector.tensor_tensor(out=flat(v[c][:, g], j0, w), in0=ag, in1=ag, op=ALU.mult)
+
+        def root(c, g):
+            vv = v[c][:, g].rearrange("p j n -> p (j n)")
+            nc.scalar.activation(out=vv, in_=vv, func=ACT.Sqrt, scale=-0.25, bias=0.25)
+
+        def drive(c, g, j):
+            col = slice(g * PACK + j, g * PACK + j + 1)
+            nc.vector.scalar_tensor_tensor(out=u[c][:, g, j, :], in0=v[c][:, g, j, :], scalar=gain_f[:, col],
+                                           in1=u[c][:, g, j, :], op0=ALU.mult, op1=ALU.mult)
+
+        tmp = {}
+
+        def recur_mul(t, g):
+            c, cols = home[t]
+            pc, pcols = home[t - 1]
+            tmp[g] = pool.tile([P, PACK, B], F32, name="tmp", bufs=4)
+            nc.vector.tensor_tensor(out=tmp[g][:], in0=a[c][:, g, :, cols], in1=u[pc][:, g, :, pcols], op=ALU.mult)
+
+        def recur_add(t, g):
+            c, cols = home[t]
+            nc.vector.tensor_tensor(out=u[c][:, g, :, cols], in0=u[c][:, g, :, cols], in1=tmp[g][:], op=ALU.add)
+
+        hb, hq, hs = {}, {}, {}
+
+        def cast_h(t):
+            c, cols = home[t]
+            hb[t] = pool.tile([P, G, B, PACK], BF16, name="hb", align_bytes=64)
+            nc.vector.tensor_copy(out=hb[t][:], in_=u[c][:, :, :, cols].rearrange("p g j n -> p g n j"))
+
+        def quantize_h(t):
+            hq[t] = pool.tile([P, G, B], I32, name="hq", bufs=4, align_bytes=64)
+            hs[t] = pool.tile([P, G, B], U8, name="hs", bufs=4, align_bytes=64)
+            nc.vector.quantize_mx(out=hq[t][:].rearrange("p g n -> p (g n)").bitcast(FP8X4),
+                                  scales=hs[t][:].rearrange("p g n -> p (g n)"),
+                                  in_=hb[t][:].rearrange("p g n j -> p (g n j)"))
+
+        osb, ob, pq = {}, {}, {}
+        psc = keep.tile([P, T, G, B], U8, name="psc", align_bytes=64)
+
+        def copy_out(engine, dst, src):
+            if engine == "a":
+                nc.scalar.copy(out=dst, in_=src)
+            else:
+                nc.vector.tensor_copy(out=dst, in_=src)
+
+        def project_rows(t, h):
+            if h == 0:
+                osb[t] = pool.tile([P, N], F32, name="osb", bufs=3)
+            bank = ps2.tile([P, 512], F32, name="bank2")
+            for k in range(G):
+                sp, row = plane["o", k]
+                nc.tensor.matmul_mx(
+                    out=bank[:], lhsT=hq[t][:, k, :].bitcast(FP8X4), lhsT_scale=hs[t][:, k, :],
+                    rhs=wp["o"][:, k, h * GC : (h + 1) * GC].bitcast(FP8X4),
+                    rhs_scale=sp[row:P, h * GC : (h + 1) * GC], start=(k == 0), stop=(k == G - 1))
+            copy_out(OE_ROW[t], osb[t][:, h * GC : (h + 1) * GC].rearrange("p (m j) -> p m j", j=PACK),
+                     bank[:].rearrange("p (j m) -> p m j", j=PACK))
+            nc.sync.dma_start(out=out_0[t][:, h * GC : (h + 1) * GC], in_=osb[t][:, h * GC : (h + 1) * GC])
+
+        def project_cols(t, h):
+            bank = ps2.tile([P, PACK, B], F32, name="bank2")
+            for j in range(PACK):
+                for k in range(G):
+                    sp, row = plane["o", k]
+                    col = h * GC + j * P
+                    nc.tensor.matmul_mx(
+                        out=bank[:, j, :], lhsT=wp["o"][:, k, col : col + P].bitcast(FP8X4),
+                        lhsT_scale=sp[row:P, col : col + P],
+                        rhs=hq[t][:, k, :].bitcast(FP8X4), rhs_scale=hs[t][:, k, :], start=(k == 0), stop=(k == G - 1))
+            if h == 0:
+                ob[t] = pool.tile([P, G, B, PACK], BF16, name="ob", bufs=4, align_bytes=64)
+            copy_out(OE_COL[t], ob[t][:, h], bank[:].rearrange("p j n -> p n j"))
+
+        def quantize_out(t):
+            pq[t] = pool.tile([P, G, B], I32, name="pq", bufs=4, align_bytes=64)
+            nc.vector.quantize_mx(out=pq[t][:].rearrange("p h n -> p (h n)").bitcast(FP8X4),
+                                  scales=psc[:, t].rearrange("p h n -> p (h n)"),
+                                  in_=ob[t][:].rearrange("p h n j -> p (h n j)"))
+            nc.sync.dma_start(out=out_1.rearrange("h p m t -> p h (m t)").bitcast(I32)[:, :, t * B : (t + 1) * B], in_=pq[t][:])
+
+        def store_scales(t0, t1):
+            for h in range(G):
+                for q in range(4):
+                    nc.sync.dma_start(out=out_2[h, 4 * q : 4 * q + 4, t0 * B : t1 * B].bitcast(I32).rearrange("r (t n) -> r t n", n=B // 4),
+                                      in_=psc[32 * q : 32 * q + 4, t0:t1, h, :].bitcast(I32))
+
+        def back(c):
+            t0, nt = CHUNKS[c]
+            out = []
+            for g in range(G):
+                for j in range(PACK):
+                    out.append(lambda g=g, j=j: drive(c, g, j))
+            for t in range(t0, t0 + nt):
+                if t:
+                    out.append(lambda t=t: [recur_mul(t, g) for g in range(G)])
+                    out.append(lambda t=t: [recur_add(t, g) for g in range(G)])
+                out.append(lambda t=t: cast_h(t))
+                out.append(lambda t=t: quantize_h(t))
+            return out
+
+        def project(t):
+            for h in range(G):
+                project_cols(t, h)
+            for h in range(G):
+                project_rows(t, h)
+
+        def steps(c):
+            return range(CHUNKS[c][0], CHUNKS[c][0] + CHUNKS[c][1])
+
+        def weave(main, extra):
+            done = 0
+            for k, f in enumerate(main):
+                f()
+                while done < len(extra) * (k + 1) // len(main):
+                    extra[done]()
+                    done += 1
+
+        load_scales("r", sraw_a, 0, nc.sync)
+        load_scales("i", sraw_a, 8, nc.sync)
+        for t in range(4):
+            load_x(t)
+        load_w("r", 0)
+        load_w("i", 0)
+        load_w("r", 1)
+        load_w("i", 1)
+        softplus_act()
+        permute_s(splane_a, sraw_a)
+        for t in range(4):
+            turn_x(t)
+            load_x(4 + t)
+            if t == 2:
+                quantize_x(0, 0, 0, 2)
+                quantize_x(0, 1, 0, 2)
+        quantize_x(0, 0, 1, 2)
+        quantize_x(0, 1, 1, 2)
+        permute_w("r", 0)
+        permute_w("i", 0)
+        softplus_vec()
+        load_scales("o", sraw_b, 0, nc.sync)
+        for h in range(G):
+            load_w("o", h)
+        early = [
+            lambda: permute_w("r", 1), lambda: permute_w("i", 1),
+            lambda: turn_x(4), lambda: turn_x(5), lambda: turn_x(6), lambda: turn_x(7),
+            lambda: quantize_x(1, 0, 0, 1), lambda: quantize_x(1, 1, 0, 1), lambda: permute_s(splane_b, sraw_b), lambda: permute_w("o", 0), lambda: permute_w("o", 1)]
+        sl = slots(0)
+        gate_matmul(0, *sl[0])
+        weave([lambda k=k: (gate_act(0, *sl[k]), [gate_matmul(0, *s) for s in sl[k + 1 : k + 2]], gate_vec(0, *sl[k])) for k in range(8)], early)
+        root(0, 0)
+        root(0, 1)
+        for s in slots(1):
+            gate_matmul(1, *s)
+            gate_act(1, *s)
+        for f in back(0):
+            f()
+        sl = slots(1)
+        for s in sl:
+            gate_vec(1, *s)
+        for t in range(4):
+            if t == ROOTAT[0]:
+                root(1, 0)
+            if t == ROOTAT[1]:
+                root(1, 1)
+            project(t)
+        pieces = back(1)
+        for f in pieces[:8]:
+            f()
+        done = 0
+        for k, f in enumerate(pieces[8:]):
+            f()
+            if k % 4 == 3:
+                t = 4 + k // 4
+                project(t)
+            if k in QOAT:
+                quantize_out(done)
+                done += 1
+        while done < T:
+            quantize_out(done)
+            done += 1
+        store_scales(0, T)

@@ -19,12 +19,14 @@ G = 2
 PACK = 4
 GC = 512
 CHUNKS = ((0, 4), (4, 4))
-SQ_ACT = ((0, 0), (0, 1))
+SQ_ACT = ((), (6, 7))
 ROOTAT = (0, 0)
+CAST = "vvvvvvv"
+XAT = (2, 3, 4, 5)
 QOAT = (1, 3, 5, 7, 10, 14)
 XE = "vavavvvv"
-OE_ROW = "aaaaaaaa"
-OE_COL = "aaaaaaaa"
+OE_ROW = ("aa",) * 8
+OE_COL = ("aa",) * 7 + ("vv",)
 XLEAD = 1
 OUTLAG = 1
 
@@ -40,18 +42,15 @@ def tile_rglrueightstepwithoutputprojection_x2_kernel(
         ps2 = ctx.enter_context(tc.psum_pool(name="ps2", bufs=4))
         ctx.enter_context(tc.manual_schedule())
 
-        sraw_a = keep.tile([P, D], U8, name="sraw_a", align_bytes=64)
-        sraw_b = keep.tile([P, D], U8, name="sraw_b", align_bytes=64)
-        splane_a = keep.tile([P, D], U8, name="splane_a", align_bytes=64)
-        splane_b = keep.tile([P, D], U8, name="splane_b", align_bytes=64)
+        sraw = {w: keep.tile([P, D], U8, name="sraw_" + w, align_bytes=64) for w in ("r", "i", "o")}
+        splane = {w: keep.tile([P, D], U8, name="splane_" + w, align_bytes=64) for w in ("r", "i", "o")}
         wp = {w: keep.tile([P, G, D], I32, name="wp_" + w, align_bytes=64) for w in ("r", "i", "o")}
-        plane = {("r", 0): (splane_a, 0), ("r", 1): (splane_a, 4), ("i", 0): (splane_a, 8), ("i", 1): (splane_a, 12),
-                 ("o", 0): (splane_b, 0), ("o", 1): (splane_b, 4)}
+        plane = {(w, g): (splane[w], 4 * g) for w in ("r", "i", "o") for g in range(G)}
         words = {"r": wr_words, "i": wi_words, "o": wo_words}
         scales = {"r": wr_scales, "i": wi_scales, "o": wo_scales}
 
-        nc.vector.memset(sraw_a[:].bitcast(I32), 0)
-        nc.vector.memset(sraw_b[:].bitcast(I32), 0)
+        for w in ("r", "i", "o"):
+            nc.gpsimd.memset(sraw[w][:].bitcast(I32), 0)
 
         lam_sb = keep.tile([P, G, PACK], BF16, name="lam_sb")
         gain_sb = keep.tile([P, G, PACK], BF16, name="gain_sb")
@@ -60,10 +59,10 @@ def tile_rglrueightstepwithoutputprojection_x2_kernel(
         ident = keep.tile([P, P], F32, name="ident")
         make_identity(nc, ident[:])
 
-        def load_scales(w, dst, row, queue):
+        def load_scales(w, queue):
             for q in range(4):
                 queue.dma_start(
-                    out=dst[32 * q + row : 32 * q + row + 8, :].bitcast(I32),
+                    out=sraw[w][32 * q : 32 * q + 8, :].bitcast(I32),
                     in_=scales[w][:, 4 * q : 4 * q + 4, :].bitcast(I32),
                 )
 
@@ -88,10 +87,11 @@ def tile_rglrueightstepwithoutputprojection_x2_kernel(
                 in_=wraw[w, h][:].rearrange("p k (m j) -> p k j m", j=PACK),
             )
 
-        def permute_s(dst, src):
+        def permute_s(w, h):
+            cols = slice(h * GC, (h + 1) * GC)
             nc.vector.tensor_copy(
-                out=dst[:].rearrange("p (h j m) -> p h j m", h=G, j=PACK),
-                in_=src[:].rearrange("p (h m j) -> p h j m", h=G, j=PACK),
+                out=splane[w][:, cols].rearrange("p (j m) -> p j m", j=PACK),
+                in_=sraw[w][:, cols].rearrange("p (m j) -> p j m", j=PACK),
             )
 
         l1 = keep.tile([P, G * PACK], F32, name="l1")
@@ -185,19 +185,23 @@ def tile_rglrueightstepwithoutputprojection_x2_kernel(
             nc.scalar.activation(out=flat(u[c][:, g], j0, w), in_=bank_i[c, g, j0][:], func=ACT.Tanh, scale=0.5)
             for j in range(j0, j0 + w):
                 col = slice(g * PACK + j, g * PACK + j + 1)
-                if SQ_ACT[c][g]:
-                    nc.scalar.activation(out=v[c][:, g, j, :], in_=a[c][:, g, j, :], func=ACT.Exp,
+                first = B if c == 0 else 0
+                sq = n if g * PACK + j0 in SQ_ACT[c] else first
+                if sq:
+                    nc.scalar.activation(out=v[c][:, g, j, :sq], in_=a[c][:, g, j, :sq], func=ACT.Exp,
                                          scale=l2[:, col], bias=l2[:, col])
-                nc.scalar.activation(out=a[c][:, g, j, :], in_=a[c][:, g, j, :], func=ACT.Exp,
+                nc.scalar.activation(out=a[c][:, g, j, first:], in_=a[c][:, g, j, first:], func=ACT.Exp,
                                      scale=l1[:, col], bias=l1[:, col])
 
         def gate_vec(c, g, j0, w):
             xb = xt_bf16(c, g).rearrange("p (n j) -> p j n", j=PACK)
             ug = u[c][:, g, j0 : j0 + w, :]
             nc.vector.scalar_tensor_tensor(out=ug, in0=ug, scalar=1.0, in1=xb[:, j0 : j0 + w, :], op0=ALU.add, op1=ALU.mult)
-            if not SQ_ACT[c][g]:
-                ag = flat(a[c][:, g], j0, w)
-                nc.vector.tensor_tensor(out=flat(v[c][:, g], j0, w), in0=ag, in1=ag, op=ALU.mult)
+
+        def square(c, g, j0, w):
+            first = B if c == 0 else 0
+            ag = a[c][:, g, j0 : j0 + w, first:]
+            nc.vector.tensor_tensor(out=v[c][:, g, j0 : j0 + w, first:], in0=ag, in1=ag, op=ALU.mult)
 
         def root(c, g):
             vv = v[c][:, g].rearrange("p j n -> p (j n)")
@@ -210,22 +214,33 @@ def tile_rglrueightstepwithoutputprojection_x2_kernel(
 
         tmp = {}
 
-        def recur_mul(t, g):
+        def recur_mul(t):
             c, cols = home[t]
             pc, pcols = home[t - 1]
-            tmp[g] = pool.tile([P, PACK, B], F32, name="tmp", bufs=4)
-            nc.vector.tensor_tensor(out=tmp[g][:], in0=a[c][:, g, :, cols], in1=u[pc][:, g, :, pcols], op=ALU.mult)
+            tmp[t] = pool.tile([P, G, PACK, B], F32, name="tmp")
+            nc.vector.tensor_tensor(
+                out=tmp[t][:].rearrange("p g j b -> p (g j) b"), in0=a[c][:].rearrange("p g j n -> p (g j) n")[:, :, cols],
+                in1=u[pc][:].rearrange("p g j n -> p (g j) n")[:, :, pcols], op=ALU.mult)
 
-        def recur_add(t, g):
+        def recur_add(t):
             c, cols = home[t]
-            nc.vector.tensor_tensor(out=u[c][:, g, :, cols], in0=u[c][:, g, :, cols], in1=tmp[g][:], op=ALU.add)
+            h = u[c][:].rearrange("p g j n -> p (g j) n")[:, :, cols]
+            nc.vector.tensor_tensor(out=h, in0=h, in1=tmp[t][:].rearrange("p g j b -> p (g j) b"), op=ALU.add)
 
         hb, hq, hs = {}, {}, {}
+
+        def recur_last(g):
+            t = T - 1
+            c, cols = home[t]
+            if g == 0:
+                hb[t] = pool.tile([P, G, B, PACK], BF16, name="hb", align_bytes=64)
+            nc.vector.tensor_tensor(out=hb[t][:, g], in0=u[c][:, g, :, cols].rearrange("p j n -> p n j"),
+                                    in1=tmp[t][:, g].rearrange("p j n -> p n j"), op=ALU.add)
 
         def cast_h(t):
             c, cols = home[t]
             hb[t] = pool.tile([P, G, B, PACK], BF16, name="hb", align_bytes=64)
-            nc.vector.tensor_copy(out=hb[t][:], in_=u[c][:, :, :, cols].rearrange("p g j n -> p g n j"))
+            copy_out(CAST[t], hb[t][:], u[c][:, :, :, cols].rearrange("p g j n -> p g n j"))
 
         def quantize_h(t):
             hq[t] = pool.tile([P, G, B], I32, name="hq", bufs=4, align_bytes=64)
@@ -235,7 +250,7 @@ def tile_rglrueightstepwithoutputprojection_x2_kernel(
                                   in_=hb[t][:].rearrange("p g n j -> p (g n j)"))
 
         osb, ob, pq = {}, {}, {}
-        psc = keep.tile([P, T, G, B], U8, name="psc", align_bytes=64)
+        psc = keep.tile([P, G, T, B], U8, name="psc", align_bytes=64)
 
         def copy_out(engine, dst, src):
             if engine == "a":
@@ -253,9 +268,12 @@ def tile_rglrueightstepwithoutputprojection_x2_kernel(
                     out=bank[:], lhsT=hq[t][:, k, :].bitcast(FP8X4), lhsT_scale=hs[t][:, k, :],
                     rhs=wp["o"][:, k, h * GC : (h + 1) * GC].bitcast(FP8X4),
                     rhs_scale=sp[row:P, h * GC : (h + 1) * GC], start=(k == 0), stop=(k == G - 1))
-            copy_out(OE_ROW[t], osb[t][:, h * GC : (h + 1) * GC].rearrange("p (m j) -> p m j", j=PACK),
+            copy_out(OE_ROW[t][h], osb[t][:, h * GC : (h + 1) * GC].rearrange("p (m j) -> p m j", j=PACK),
                      bank[:].rearrange("p (j m) -> p m j", j=PACK))
-            nc.sync.dma_start(out=out_0[t][:, h * GC : (h + 1) * GC], in_=osb[t][:, h * GC : (h + 1) * GC])
+            if t >= T - 2:
+                nc.sync.dma_start(out=out_0[t][:, h * GC : (h + 1) * GC], in_=osb[t][:, h * GC : (h + 1) * GC])
+            elif h == G - 1:
+                nc.sync.dma_start(out=out_0[t], in_=osb[t][:])
 
         def project_cols(t, h):
             bank = ps2.tile([P, PACK, B], F32, name="bank2")
@@ -269,40 +287,29 @@ def tile_rglrueightstepwithoutputprojection_x2_kernel(
                         rhs=hq[t][:, k, :].bitcast(FP8X4), rhs_scale=hs[t][:, k, :], start=(k == 0), stop=(k == G - 1))
             if h == 0:
                 ob[t] = pool.tile([P, G, B, PACK], BF16, name="ob", bufs=4, align_bytes=64)
-            copy_out(OE_COL[t], ob[t][:, h], bank[:].rearrange("p j n -> p n j"))
+            copy_out(OE_COL[t][h], ob[t][:, h], bank[:].rearrange("p j n -> p n j"))
 
         def quantize_out(t):
             pq[t] = pool.tile([P, G, B], I32, name="pq", bufs=4, align_bytes=64)
-            nc.vector.quantize_mx(out=pq[t][:].rearrange("p h n -> p (h n)").bitcast(FP8X4),
-                                  scales=psc[:, t].rearrange("p h n -> p (h n)"),
-                                  in_=ob[t][:].rearrange("p h n j -> p (h n j)"))
+            for h in range(G):
+                nc.vector.quantize_mx(out=pq[t][:, h, :].bitcast(FP8X4), scales=psc[:, h, t, :],
+                                      in_=ob[t][:, h].rearrange("p n j -> p (n j)"))
             nc.sync.dma_start(out=out_1.rearrange("h p m t -> p h (m t)").bitcast(I32)[:, :, t * B : (t + 1) * B], in_=pq[t][:])
 
-        def store_scales(t0, t1):
-            for h in range(G):
-                for q in range(4):
-                    nc.sync.dma_start(out=out_2[h, 4 * q : 4 * q + 4, t0 * B : t1 * B].bitcast(I32).rearrange("r (t n) -> r t n", n=B // 4),
-                                      in_=psc[32 * q : 32 * q + 4, t0:t1, h, :].bitcast(I32))
-
-        def back(c):
-            t0, nt = CHUNKS[c]
-            out = []
-            for g in range(G):
-                for j in range(PACK):
-                    out.append(lambda g=g, j=j: drive(c, g, j))
-            for t in range(t0, t0 + nt):
-                if t:
-                    out.append(lambda t=t: [recur_mul(t, g) for g in range(G)])
-                    out.append(lambda t=t: [recur_add(t, g) for g in range(G)])
-                out.append(lambda t=t: cast_h(t))
-                out.append(lambda t=t: quantize_h(t))
-            return out
+        def store_scales(t0, t1, queue):
+            for q in range(4):
+                queue.dma_start(
+                    out=out_2[:, 4 * q : 4 * q + 4, t0 * B : t1 * B].bitcast(I32).rearrange("h r n -> r h n"),
+                    in_=psc[32 * q : 32 * q + 4, :, t0:t1, :].rearrange("r h t n -> r h (t n)").bitcast(I32))
 
         def project(t):
             for h in range(G):
                 project_cols(t, h)
             for h in range(G):
                 project_rows(t, h)
+
+        def spread(items, n):
+            return [items[k * len(items) // n : (k + 1) * len(items) // n] for k in range(n)]
 
         def steps(c):
             return range(CHUNKS[c][0], CHUNKS[c][0] + CHUNKS[c][1])
@@ -315,66 +322,118 @@ def tile_rglrueightstepwithoutputprojection_x2_kernel(
                     extra[done]()
                     done += 1
 
-        load_scales("r", sraw_a, 0, nc.sync)
-        load_scales("i", sraw_a, 8, nc.sync)
         for t in range(4):
             load_x(t)
         load_w("r", 0)
         load_w("i", 0)
+        load_scales("r", nc.gpsimd)
+        load_scales("i", nc.sync)
         load_w("r", 1)
         load_w("i", 1)
         softplus_act()
-        permute_s(splane_a, sraw_a)
         for t in range(4):
             turn_x(t)
             load_x(4 + t)
             if t == 2:
+                pass
+            if t == 3:
                 quantize_x(0, 0, 0, 2)
                 quantize_x(0, 1, 0, 2)
         quantize_x(0, 0, 1, 2)
         quantize_x(0, 1, 1, 2)
         permute_w("r", 0)
+        permute_s("r", 0)
         permute_w("i", 0)
+        permute_s("i", 0)
         softplus_vec()
-        load_scales("o", sraw_b, 0, nc.sync)
+        load_scales("o", nc.sync)
         for h in range(G):
             load_w("o", h)
         early = [
-            lambda: permute_w("r", 1), lambda: permute_w("i", 1),
+            lambda: (permute_w("r", 1), permute_s("r", 1)), lambda: (permute_w("i", 1), permute_s("i", 1)),
             lambda: turn_x(4), lambda: turn_x(5), lambda: turn_x(6), lambda: turn_x(7),
-            lambda: quantize_x(1, 0, 0, 1), lambda: quantize_x(1, 1, 0, 1), lambda: permute_s(splane_b, sraw_b), lambda: permute_w("o", 0), lambda: permute_w("o", 1)]
+            lambda: quantize_x(1, 0, 0, 1), lambda: quantize_x(1, 1, 0, 1),
+            lambda: (permute_s("o", 0), permute_s("o", 1)), lambda: permute_w("o", 0), lambda: permute_w("o", 1)]
         sl = slots(0)
         gate_matmul(0, *sl[0])
-        weave([lambda k=k: (gate_act(0, *sl[k]), [gate_matmul(0, *s) for s in sl[k + 1 : k + 2]], gate_vec(0, *sl[k])) for k in range(8)], early)
+        es = spread(early, 8)
+        for k in range(8):
+            gate_act(0, *sl[k])
+            if k < 7:
+                gate_matmul(0, *sl[k + 1])
+            if k % 2:
+                gate_vec(0, sl[k][0], sl[k][1] - 1, 2)
+                if k < 7:
+                    square(0, sl[k][0], sl[k][1] - 1, 2)
+            if k >= 6:
+                square(0, sl[k][0], sl[k][1], 1)
+            for f in es[k]:
+                f()
         root(0, 0)
         root(0, 1)
-        for s in slots(1):
-            gate_matmul(1, *s)
-            gate_act(1, *s)
-        for f in back(0):
-            f()
         sl = slots(1)
         for s in sl:
-            gate_vec(1, *s)
+            gate_matmul(1, *s)
+            gate_act(1, *s)
+
+        def drive_all(c):
+            for g in range(G):
+                for j in range(PACK):
+                    drive(c, g, j)
+
+        nsq = PACK * G - len(SQ_ACT[1])
+        drive_all(0)
+        cast_h(0)
+        for t in range(1, 4):
+            recur_mul(t)
+            quantize_h(t - 1)
+            recur_add(t)
+            if t == 1:
+                gate_vec(1, 0, 0, 2)
+            if t == 2:
+                square(1, 0, 0, 2)
+            if t == 3:
+                gate_vec(1, 0, 2, 2)
+            cast_h(t)
+        square(1, 0, 2, 2)
+        quantize_h(3)
+        if nsq > 4:
+            square(1, 1, 0, nsq - 4)
+        gate_vec(1, 1, 0, 4)
         for t in range(4):
             if t == ROOTAT[0]:
                 root(1, 0)
             if t == ROOTAT[1]:
                 root(1, 1)
             project(t)
-        pieces = back(1)
-        for f in pieces[:8]:
-            f()
-        done = 0
-        for k, f in enumerate(pieces[8:]):
-            f()
-            if k % 4 == 3:
-                t = 4 + k // 4
-                project(t)
-            if k in QOAT:
-                quantize_out(done)
-                done += 1
-        while done < T:
-            quantize_out(done)
-            done += 1
-        store_scales(0, T)
+        drive_all(1)
+        recur_mul(4)
+        quantize_out(0)
+        recur_add(4)
+        quantize_out(1)
+        recur_mul(5)
+        cast_h(4)
+        recur_add(5)
+        quantize_h(4)
+        project(4)
+        quantize_out(2)
+        recur_mul(6)
+        cast_h(5)
+        recur_add(6)
+        quantize_h(5)
+        project(5)
+        quantize_out(3)
+        recur_mul(7)
+        cast_h(6)
+        quantize_out(4)
+        quantize_h(6)
+        recur_last(0)
+        recur_last(1)
+        quantize_out(5)
+        store_scales(0, 6, nc.sync)
+        quantize_h(7)
+        project(6)
+        project(7)
+        quantize_out(6)
+        quantize_out(7)
+        store_scales(6, 8, nc.scalar)

@@ -19,12 +19,14 @@ G = 2
 PACK = 4
 GC = 512
 CHUNKS = ((0, 4), (4, 4))
-SQ_ACT = ((), (6, 7))
+SQ_ACT = ((), (5, 6, 7))
 ROOTAT = (0, 0)
-CAST = "vvvvvvv"
+CAST = ("vv",) * 7
+FIRST = B
+RP = 2
 XAT = (2, 3, 4, 5)
 QOAT = (1, 3, 5, 7, 10, 14)
-XE = "vavavvvv"
+XE = "vaaavvvv"
 OE_ROW = ("aa",) * 8
 OE_COL = ("aa",) * 7 + ("vv",)
 XLEAD = 1
@@ -42,35 +44,38 @@ def tile_rglrueightstepwithoutputprojection_x2_kernel(
         ps2 = ctx.enter_context(tc.psum_pool(name="ps2", bufs=4))
         ctx.enter_context(tc.manual_schedule())
 
-        sraw = {w: keep.tile([P, D], U8, name="sraw_" + w, align_bytes=64) for w in ("r", "i", "o")}
-        splane = {w: keep.tile([P, D], U8, name="splane_" + w, align_bytes=64) for w in ("r", "i", "o")}
+        sraw = {w: keep.tile([P, D], U8, name="sraw_" + w, align_bytes=64) for w in ("g", "o")}
+        splane = {w: keep.tile([P, D], U8, name="splane_" + w, align_bytes=64) for w in ("g", "o")}
         wp = {w: keep.tile([P, G, D], I32, name="wp_" + w, align_bytes=64) for w in ("r", "i", "o")}
-        plane = {(w, g): (splane[w], 4 * g) for w in ("r", "i", "o") for g in range(G)}
+        place = {"r": ("g", 0), "i": ("g", 8), "o": ("o", 0)}
+        plane = {(w, g): (splane[place[w][0]], place[w][1] + 4 * g) for w in ("r", "i", "o") for g in range(G)}
         words = {"r": wr_words, "i": wi_words, "o": wo_words}
         scales = {"r": wr_scales, "i": wi_scales, "o": wo_scales}
 
-        for w in ("r", "i", "o"):
-            nc.gpsimd.memset(sraw[w][:].bitcast(I32), 0)
+        for w in ("g", "o"):
+            nc.vector.memset(sraw[w][:].bitcast(I32), 0)
 
         lam_sb = keep.tile([P, G, PACK], BF16, name="lam_sb")
         gain_sb = keep.tile([P, G, PACK], BF16, name="gain_sb")
         nc.scalar.dma_start(out=lam_sb[:], in_=lam.rearrange("(g p j) -> p g j", g=G, j=PACK))
-        nc.scalar.dma_start(out=gain_sb[:], in_=gain.rearrange("(g p j) -> p g j", g=G, j=PACK))
+        nc.gpsimd.dma_start(out=gain_sb[:], in_=gain.rearrange("(g p j) -> p g j", g=G, j=PACK))
         ident = keep.tile([P, P], F32, name="ident")
         make_identity(nc, ident[:])
 
         def load_scales(w, queue):
             for q in range(4):
+                s, row = place[w]
                 queue.dma_start(
-                    out=sraw[w][32 * q : 32 * q + 8, :].bitcast(I32),
+                    out=sraw[s][32 * q + row : 32 * q + row + 8, :].bitcast(I32),
                     in_=scales[w][:, 4 * q : 4 * q + 4, :].bitcast(I32),
                 )
 
         xraw = {}
 
         def load_x(t):
-            xraw[t] = pool.tile([P, D], BF16, name="xraw", bufs=4)
-            nc.sync.dma_start(out=xraw[t][:], in_=x[t])
+            pair = pool.tile([P, 2, D], BF16, name="xraw")
+            nc.sync.dma_start(out=pair[:], in_=x[t : t + 2].rearrange("t b d -> b t d"))
+            xraw[t], xraw[t + 1] = pair[:, 0, :], pair[:, 1, :]
 
         wraw = {}
 
@@ -127,7 +132,7 @@ def tile_rglrueightstepwithoutputprojection_x2_kernel(
             if t == t0:
                 xt4[c] = pool.tile([P, G, nt * B, 2], F32, name="xt4", align_bytes=64)
             bank = ps2.tile([P, G, 2, B], F32, name="bank2")
-            w32 = xraw[t][:].bitcast(F32)
+            w32 = xraw[t].bitcast(F32)
             for g in range(G):
                 for u in range(2):
                     nc.tensor.transpose(bank[:, g, u, :], w32[:, 256 * g + u : 256 * (g + 1) : 2], ident[:])
@@ -185,7 +190,7 @@ def tile_rglrueightstepwithoutputprojection_x2_kernel(
             nc.scalar.activation(out=flat(u[c][:, g], j0, w), in_=bank_i[c, g, j0][:], func=ACT.Tanh, scale=0.5)
             for j in range(j0, j0 + w):
                 col = slice(g * PACK + j, g * PACK + j + 1)
-                first = B if c == 0 else 0
+                first = FIRST if c == 0 else 0
                 sq = n if g * PACK + j0 in SQ_ACT[c] else first
                 if sq:
                     nc.scalar.activation(out=v[c][:, g, j, :sq], in_=a[c][:, g, j, :sq], func=ACT.Exp,
@@ -199,13 +204,14 @@ def tile_rglrueightstepwithoutputprojection_x2_kernel(
             nc.vector.scalar_tensor_tensor(out=ug, in0=ug, scalar=1.0, in1=xb[:, j0 : j0 + w, :], op0=ALU.add, op1=ALU.mult)
 
         def square(c, g, j0, w):
-            first = B if c == 0 else 0
+            first = FIRST if c == 0 else 0
             ag = a[c][:, g, j0 : j0 + w, first:]
             nc.vector.tensor_tensor(out=v[c][:, g, j0 : j0 + w, first:], in0=ag, in1=ag, op=ALU.mult)
 
         def root(c, g):
-            vv = v[c][:, g].rearrange("p j n -> p (j n)")
-            nc.scalar.activation(out=vv, in_=vv, func=ACT.Sqrt, scale=-0.25, bias=0.25)
+            for j in range(0, PACK, RP):
+                vv = flat(v[c][:, g], j, RP)
+                nc.scalar.activation(out=vv, in_=vv, func=ACT.Sqrt, scale=-0.25, bias=0.25)
 
         def drive(c, g, j):
             col = slice(g * PACK + j, g * PACK + j + 1)
@@ -240,7 +246,11 @@ def tile_rglrueightstepwithoutputprojection_x2_kernel(
         def cast_h(t):
             c, cols = home[t]
             hb[t] = pool.tile([P, G, B, PACK], BF16, name="hb", align_bytes=64)
-            copy_out(CAST[t], hb[t][:], u[c][:, :, :, cols].rearrange("p g j n -> p g n j"))
+            if CAST[t] == "vv":
+                copy_out("v", hb[t][:], u[c][:, :, :, cols].rearrange("p g j n -> p g n j"))
+            else:
+                for g in range(G):
+                    copy_out(CAST[t][g], hb[t][:, g], u[c][:, g, :, cols].rearrange("p j n -> p n j"))
 
         def quantize_h(t):
             hq[t] = pool.tile([P, G, B], I32, name="hq", bufs=4, align_bytes=64)
@@ -270,7 +280,7 @@ def tile_rglrueightstepwithoutputprojection_x2_kernel(
                     rhs_scale=sp[row:P, h * GC : (h + 1) * GC], start=(k == 0), stop=(k == G - 1))
             copy_out(OE_ROW[t][h], osb[t][:, h * GC : (h + 1) * GC].rearrange("p (m j) -> p m j", j=PACK),
                      bank[:].rearrange("p (j m) -> p m j", j=PACK))
-            if t >= T - 2:
+            if t == T - 1:
                 nc.sync.dma_start(out=out_0[t][:, h * GC : (h + 1) * GC], in_=osb[t][:, h * GC : (h + 1) * GC])
             elif h == G - 1:
                 nc.sync.dma_start(out=out_0[t], in_=osb[t][:])
@@ -322,38 +332,37 @@ def tile_rglrueightstepwithoutputprojection_x2_kernel(
                     extra[done]()
                     done += 1
 
-        for t in range(4):
-            load_x(t)
+        load_x(0)
+        load_scales("r", nc.sync)
         load_w("r", 0)
-        load_w("i", 0)
-        load_scales("r", nc.gpsimd)
+        load_x(2)
         load_scales("i", nc.sync)
+        load_w("i", 0)
         load_w("r", 1)
         load_w("i", 1)
         softplus_act()
-        for t in range(4):
-            turn_x(t)
-            load_x(4 + t)
-            if t == 2:
-                pass
-            if t == 3:
-                quantize_x(0, 0, 0, 2)
-                quantize_x(0, 1, 0, 2)
+        turn_x(0)
+        turn_x(1)
+        load_x(4)
+        quantize_x(0, 0, 0, 2)
+        quantize_x(0, 1, 0, 2)
+        permute_w("r", 0)
+        permute_s("g", 0)
+        turn_x(2)
+        turn_x(3)
+        load_x(6)
         quantize_x(0, 0, 1, 2)
         quantize_x(0, 1, 1, 2)
-        permute_w("r", 0)
-        permute_s("r", 0)
         permute_w("i", 0)
-        permute_s("i", 0)
         softplus_vec()
         load_scales("o", nc.sync)
         for h in range(G):
             load_w("o", h)
         early = [
-            lambda: (permute_w("r", 1), permute_s("r", 1)), lambda: (permute_w("i", 1), permute_s("i", 1)),
-            lambda: turn_x(4), lambda: turn_x(5), lambda: turn_x(6), lambda: turn_x(7),
+            lambda: (permute_w("r", 1), permute_s("g", 1)), lambda: permute_w("i", 1),
+            lambda: (turn_x(4), turn_x(5)), lambda: (turn_x(6), turn_x(7)),
             lambda: quantize_x(1, 0, 0, 1), lambda: quantize_x(1, 1, 0, 1),
-            lambda: (permute_s("o", 0), permute_s("o", 1)), lambda: permute_w("o", 0), lambda: permute_w("o", 1)]
+            lambda: (permute_s("o", 0), permute_s("o", 1)), lambda: permute_w("o", 0)]
         sl = slots(0)
         gate_matmul(0, *sl[0])
         es = spread(early, 8)
@@ -383,6 +392,7 @@ def tile_rglrueightstepwithoutputprojection_x2_kernel(
 
         nsq = PACK * G - len(SQ_ACT[1])
         drive_all(0)
+        permute_w("o", 1)
         cast_h(0)
         for t in range(1, 4):
             recur_mul(t)
@@ -425,15 +435,15 @@ def tile_rglrueightstepwithoutputprojection_x2_kernel(
         quantize_out(3)
         recur_mul(7)
         cast_h(6)
-        quantize_out(4)
-        quantize_h(6)
         recur_last(0)
+        quantize_h(6)
         recur_last(1)
+        quantize_out(4)
+        quantize_h(7)
         quantize_out(5)
         store_scales(0, 6, nc.sync)
-        quantize_h(7)
         project(6)
         project(7)
         quantize_out(6)
         quantize_out(7)
-        store_scales(6, 8, nc.scalar)
+        store_scales(6, 8, nc.sync)

@@ -19,7 +19,7 @@ G = 2
 PACK = 4
 GC = 512
 CHUNKS = ((0, 4), (4, 4))
-SQ_ACT = ((), (5, 6, 7))
+SQ_ACT = ((), (6, 7))
 ROOTAT = (0, 0)
 CAST = ("vv",) * 7
 FIRST = B
@@ -88,8 +88,8 @@ def tile_rglrueightstepwithoutputprojection_x2_kernel(
 
         def permute_w(w, h):
             nc.vector.tensor_copy(
-                out=wp[w][:, :, h * GC : (h + 1) * GC].rearrange("p k (j m) -> p k j m", j=PACK),
-                in_=wraw[w, h][:].rearrange("p k (m j) -> p k j m", j=PACK),
+                out=wp[w][:, :, h * GC : (h + 1) * GC].rearrange("p k (j m) -> p k m j", j=PACK),
+                in_=wraw[w, h][:].rearrange("p k (m j) -> p k m j", j=PACK),
             )
 
         def permute_s(w, h):
@@ -240,24 +240,24 @@ def tile_rglrueightstepwithoutputprojection_x2_kernel(
             c, cols = home[t]
             if g == 0:
                 hb[t] = pool.tile([P, G, B, PACK], BF16, name="hb", align_bytes=64)
-            nc.vector.tensor_tensor(out=hb[t][:, g], in0=u[c][:, g, :, cols].rearrange("p j n -> p n j"),
-                                    in1=tmp[t][:, g].rearrange("p j n -> p n j"), op=ALU.add)
+            nc.vector.tensor_tensor(out=hb[t][:, g].rearrange("p (n i) j -> p n j i", i=4),
+                                    in0=u[c][:, g, :, cols].rearrange("p j (n i) -> p n j i", i=4),
+                                    in1=tmp[t][:, g].rearrange("p j (n i) -> p n j i", i=4), op=ALU.add)
 
         def cast_h(t):
             c, cols = home[t]
             hb[t] = pool.tile([P, G, B, PACK], BF16, name="hb", align_bytes=64)
-            if CAST[t] == "vv":
-                copy_out("v", hb[t][:], u[c][:, :, :, cols].rearrange("p g j n -> p g n j"))
-            else:
-                for g in range(G):
-                    copy_out(CAST[t][g], hb[t][:, g], u[c][:, g, :, cols].rearrange("p j n -> p n j"))
+            for g in range(G):
+                copy_out(CAST[t][g], hb[t][:, g].rearrange("p (n i) j -> p n j i", i=4),
+                         u[c][:, g, :, cols].rearrange("p j (n i) -> p n j i", i=4))
 
-        def quantize_h(t):
+        def quantize_h(t, split=False):
             hq[t] = pool.tile([P, G, B], I32, name="hq", bufs=4, align_bytes=64)
             hs[t] = pool.tile([P, G, B], U8, name="hs", bufs=4, align_bytes=64)
-            nc.vector.quantize_mx(out=hq[t][:].rearrange("p g n -> p (g n)").bitcast(FP8X4),
-                                  scales=hs[t][:].rearrange("p g n -> p (g n)"),
-                                  in_=hb[t][:].rearrange("p g n j -> p (g n j)"))
+            for gs in ((slice(0, 1), slice(1, 2)) if split else (slice(0, 2),)):
+                nc.vector.quantize_mx(out=hq[t][:, gs].rearrange("p g n -> p (g n)").bitcast(FP8X4),
+                                      scales=hs[t][:, gs].rearrange("p g n -> p (g n)"),
+                                      in_=hb[t][:, gs].rearrange("p g n j -> p (g n j)"))
 
         osb, ob, pq = {}, {}, {}
         psc = keep.tile([P, G, T, B], U8, name="psc", align_bytes=64)
@@ -271,7 +271,7 @@ def tile_rglrueightstepwithoutputprojection_x2_kernel(
         def project_rows(t, h):
             if h == 0:
                 osb[t] = pool.tile([P, N], F32, name="osb", bufs=3)
-            bank = ps2.tile([P, 512], F32, name="bank2")
+            bank = ps1.tile([P, 512], F32, name="bank1")
             for k in range(G):
                 sp, row = plane["o", k]
                 nc.tensor.matmul_mx(
@@ -300,11 +300,15 @@ def tile_rglrueightstepwithoutputprojection_x2_kernel(
             copy_out(OE_COL[t][h], ob[t][:, h], bank[:].rearrange("p j n -> p n j"))
 
         def quantize_out(t):
-            pq[t] = pool.tile([P, G, B], I32, name="pq", bufs=4, align_bytes=64)
+            if t % 2 == 0:
+                pq[t] = pool.tile([P, G, 2, B], I32, name="pq", align_bytes=64)
+            dst = pq[t - t % 2]
             for h in range(G):
-                nc.vector.quantize_mx(out=pq[t][:, h, :].bitcast(FP8X4), scales=psc[:, h, t, :],
+                nc.vector.quantize_mx(out=dst[:, h, t % 2, :].bitcast(FP8X4), scales=psc[:, h, t, :],
                                       in_=ob[t][:, h].rearrange("p n j -> p (n j)"))
-            nc.sync.dma_start(out=out_1.rearrange("h p m t -> p h (m t)").bitcast(I32)[:, :, t * B : (t + 1) * B], in_=pq[t][:])
+            if t % 2:
+                nc.sync.dma_start(out=out_1.rearrange("h p m t -> p h (m t)").bitcast(I32)[:, :, (t - 1) * B : (t + 1) * B],
+                                  in_=dst[:].rearrange("p h t b -> p h (t b)"))
 
         def store_scales(t0, t1, queue):
             for q in range(4):
@@ -433,17 +437,17 @@ def tile_rglrueightstepwithoutputprojection_x2_kernel(
         quantize_h(5)
         project(5)
         quantize_out(3)
+        store_scales(0, 4, nc.sync)
         recur_mul(7)
         cast_h(6)
+        quantize_h(6, True)
         recur_last(0)
-        quantize_h(6)
         recur_last(1)
+        quantize_h(7, True)
         quantize_out(4)
-        quantize_h(7)
         quantize_out(5)
-        store_scales(0, 6, nc.sync)
         project(6)
         project(7)
         quantize_out(6)
         quantize_out(7)
-        store_scales(6, 8, nc.sync)
+        store_scales(4, 8, nc.sync)

@@ -15,22 +15,13 @@ ACT = mybir.ActivationFunctionType
 ALU = mybir.AluOpType
 
 P = 128
-G = 2
-PACK = 4
-GC = 512
-CHUNKS = ((0, 4), (4, 4))
-SQ_ACT = ((), (6, 7))
-ROOTAT = (0, 0)
-CAST = ("vv",) * 7
-FIRST = B
-RP = 2
-XAT = (2, 3, 4, 5)
-QOAT = (1, 3, 5, 7, 10, 14)
-XE = "vaaavvvv"
-OE_ROW = ("aa",) * 8
-OE_COL = ("aa",) * 7 + ("vv",)
-XLEAD = 1
-OUTLAG = 1
+LANES = 4
+GROUP = P * LANES
+G = D // GROUP
+HALF = 4
+BANK = 512
+QUADRANT = 32
+SQUARES_ON_SCALAR = ((1, 1, 2), (1, 1, 3))
 
 
 def tile_rglrueightstepwithoutputprojection_x2_kernel(
@@ -40,414 +31,478 @@ def tile_rglrueightstepwithoutputprojection_x2_kernel(
     with ExitStack() as ctx:
         keep = ctx.enter_context(tc.tile_pool(name="keep", bufs=1))
         pool = ctx.enter_context(tc.tile_pool(name="pool", bufs=2))
-        ps1 = ctx.enter_context(tc.psum_pool(name="ps1", bufs=4))
-        ps2 = ctx.enter_context(tc.psum_pool(name="ps2", bufs=4))
+        psum_a = ctx.enter_context(tc.psum_pool(name="psum_a", bufs=4))
+        psum_b = ctx.enter_context(tc.psum_pool(name="psum_b", bufs=4))
         ctx.enter_context(tc.manual_schedule())
 
-        sraw = {w: keep.tile([P, D], U8, name="sraw_" + w, align_bytes=64) for w in ("g", "o")}
-        splane = {w: keep.tile([P, D], U8, name="splane_" + w, align_bytes=64) for w in ("g", "o")}
-        wp = {w: keep.tile([P, G, D], I32, name="wp_" + w, align_bytes=64) for w in ("r", "i", "o")}
-        place = {"r": ("g", 0), "i": ("g", 8), "o": ("o", 0)}
-        plane = {(w, g): (splane[place[w][0]], place[w][1] + 4 * g) for w in ("r", "i", "o") for g in range(G)}
+        arrived_scales = {s: keep.tile([P, D], U8, name="arrived_scales_" + s, align_bytes=64) for s in ("gates", "out")}
+        moved_scales = {s: keep.tile([P, D], U8, name="moved_scales_" + s, align_bytes=64) for s in ("gates", "out")}
+        moved_words = {w: keep.tile([P, G, D], I32, name="moved_words_" + w, align_bytes=64) for w in ("r", "i", "o")}
+        scale_place = {"r": ("gates", 0), "i": ("gates", 8), "o": ("out", 0)}
         words = {"r": wr_words, "i": wi_words, "o": wo_words}
         scales = {"r": wr_scales, "i": wi_scales, "o": wo_scales}
 
-        for w in ("g", "o"):
-            nc.vector.memset(sraw[w][:].bitcast(I32), 0)
+        for s in ("gates", "out"):
+            nc.vector.memset(arrived_scales[s][:].bitcast(I32), 0)
 
-        lam_sb = keep.tile([P, G, PACK], BF16, name="lam_sb")
-        gain_sb = keep.tile([P, G, PACK], BF16, name="gain_sb")
-        nc.scalar.dma_start(out=lam_sb[:], in_=lam.rearrange("(g p j) -> p g j", g=G, j=PACK))
-        nc.gpsimd.dma_start(out=gain_sb[:], in_=gain.rearrange("(g p j) -> p g j", g=G, j=PACK))
-        ident = keep.tile([P, P], F32, name="ident")
-        make_identity(nc, ident[:])
+        lam_in = keep.tile([P, G, LANES], BF16, name="lam_in")
+        gain_in = keep.tile([P, G, LANES], BF16, name="gain_in")
+        nc.scalar.dma_start(out=lam_in[:], in_=lam.rearrange("(g p j) -> p g j", g=G, j=LANES))
+        nc.gpsimd.dma_start(out=gain_in[:], in_=gain.rearrange("(g p j) -> p g j", g=G, j=LANES))
+        identity = keep.tile([P, P], F32, name="identity")
+        make_identity(nc, identity[:])
 
-        def load_scales(w, queue):
-            for q in range(4):
-                s, row = place[w]
-                queue.dma_start(
-                    out=sraw[s][32 * q + row : 32 * q + row + 8, :].bitcast(I32),
+        def load_scale_rows(w):
+            s, first_row = scale_place[w]
+            for q in range(P // QUADRANT):
+                row = QUADRANT * q + first_row
+                nc.sync.dma_start(
+                    out=arrived_scales[s][row : row + 4 * G, :].bitcast(I32),
                     in_=scales[w][:, 4 * q : 4 * q + 4, :].bitcast(I32),
                 )
 
-        xraw = {}
+        arrived_words = {}
+
+        def load_words(w, h):
+            arrived_words[w, h] = pool.tile([P, G, GROUP], I32, name="arrived_words", bufs=4)
+            nc.sync.dma_start(
+                out=arrived_words[w, h][:],
+                in_=words[w].rearrange("k p n t -> p k (n t)").bitcast(I32)[:, :, h * GROUP : (h + 1) * GROUP],
+            )
+
+        def move_words(w, h):
+            nc.vector.tensor_copy(
+                out=moved_words[w][:, :, h * GROUP : (h + 1) * GROUP].rearrange("p k (j m) -> p k m j", j=LANES),
+                in_=arrived_words[w, h][:].rearrange("p k (m j) -> p k m j", j=LANES),
+            )
+
+        def move_scales(s, h):
+            cols = slice(h * GROUP, (h + 1) * GROUP)
+            nc.vector.tensor_copy(
+                out=moved_scales[s][:, cols].rearrange("p (j m) -> p j m", j=LANES),
+                in_=arrived_scales[s][:, cols].rearrange("p (m j) -> p j m", j=LANES),
+            )
+
+        def weight(w, k, first, width):
+            s, first_row = scale_place[w]
+            cols = slice(first, first + width)
+            return moved_words[w][:, k, cols].bitcast(FP8X4), moved_scales[s][first_row + 4 * k : P, cols]
+
+        log_a = keep.tile([P, G * LANES], F32, name="log_a")
+        log_a_twice = keep.tile([P, G * LANES], F32, name="log_a_twice")
+        gain_f = keep.tile([P, G * LANES], F32, name="gain_f")
+        lam_flat = lam_in[:].rearrange("p g j -> p (g j)")
+        log_term = keep.tile([P, G * LANES], F32, name="log_term")
+        softplus = keep.tile([P, G * LANES], F32, name="softplus")
+
+        def channel_constants_on_scalar():
+            nc.scalar.activation(out=log_term[:], in_=lam_flat, func=ACT.Abs)
+            nc.scalar.activation(out=log_term[:], in_=log_term[:], func=ACT.Exp, scale=-1.0)
+            nc.scalar.activation(out=log_term[:], in_=log_term[:], func=ACT.Ln, bias=1.0)
+
+        def channel_constants_on_gpsimd():
+            nc.gpsimd.tensor_scalar_max(softplus[:], lam_flat, 0.0)
+            nc.gpsimd.tensor_tensor(out=softplus[:], in0=softplus[:], in1=log_term[:], op=ALU.add)
+            nc.gpsimd.tensor_scalar_mul(log_a[:], softplus[:], -4.0)
+            nc.gpsimd.tensor_scalar_mul(log_a_twice[:], softplus[:], -8.0)
+            nc.gpsimd.tensor_copy(out=gain_f[:], in_=gain_in[:].rearrange("p g j -> p (g j)"))
+
+        def of_channel(values, g, j):
+            return values[:, g * LANES + j : g * LANES + j + 1]
+
+        def in_half(t, steps=1):
+            return slice((t % HALF) * B, (t % HALF + steps) * B)
+
+        arrived_x, turned_bank, x_words, x_codes, x_scales = {}, {}, {}, {}, {}
 
         def load_x(t):
-            pair = pool.tile([P, 2, D], BF16, name="xraw")
+            pair = pool.tile([P, 2, D], BF16, name="arrived_x")
             nc.sync.dma_start(out=pair[:], in_=x[t : t + 2].rearrange("t b d -> b t d"))
-            xraw[t], xraw[t + 1] = pair[:, 0, :], pair[:, 1, :]
-
-        wraw = {}
-
-        def load_w(w, h):
-            wraw[w, h] = pool.tile([P, G, GC], I32, name="wraw", bufs=4)
-            nc.sync.dma_start(
-                out=wraw[w, h][:],
-                in_=words[w].rearrange("g p n t -> p g (n t)").bitcast(I32)[:, :, h * GC : (h + 1) * GC],
-            )
-
-        def permute_w(w, h):
-            nc.vector.tensor_copy(
-                out=wp[w][:, :, h * GC : (h + 1) * GC].rearrange("p k (j m) -> p k m j", j=PACK),
-                in_=wraw[w, h][:].rearrange("p k (m j) -> p k m j", j=PACK),
-            )
-
-        def permute_s(w, h):
-            cols = slice(h * GC, (h + 1) * GC)
-            nc.vector.tensor_copy(
-                out=splane[w][:, cols].rearrange("p (j m) -> p j m", j=PACK),
-                in_=sraw[w][:, cols].rearrange("p (m j) -> p j m", j=PACK),
-            )
-
-        l1 = keep.tile([P, G * PACK], F32, name="l1")
-        l2 = keep.tile([P, G * PACK], F32, name="l2")
-        gain_f = keep.tile([P, G * PACK], F32, name="gain_f")
-
-        lam2 = lam_sb[:].rearrange("p g j -> p (g j)")
-        mag = keep.tile([P, G * PACK], F32, name="mag")
-        pos = keep.tile([P, G * PACK], F32, name="pos")
-
-        def softplus_act():
-            nc.scalar.activation(out=mag[:], in_=lam2, func=ACT.Abs)
-            nc.scalar.activation(out=mag[:], in_=mag[:], func=ACT.Exp, scale=-1.0)
-            nc.scalar.activation(out=mag[:], in_=mag[:], func=ACT.Ln, bias=1.0)
-
-        def softplus_vec():
-            nc.vector.tensor_copy(out=gain_f[:], in_=gain_sb[:].rearrange("p g j -> p (g j)"))
-            nc.vector.tensor_scalar_max(pos[:], lam2, 0.0)
-            nc.vector.tensor_tensor(out=pos[:], in0=pos[:], in1=mag[:], op=ALU.add)
-            nc.vector.tensor_scalar_mul(l1[:], pos[:], -4.0)
-            nc.vector.tensor_scalar_mul(l2[:], pos[:], -8.0)
-
-        home = {}
-        for c, (t0, nt) in enumerate(CHUNKS):
-            for k in range(nt):
-                home[t0 + k] = (c, slice(k * B, (k + 1) * B))
-
-        xt4, xq, xs = {}, {}, {}
+            arrived_x[t], arrived_x[t + 1] = pair[:, 0, :], pair[:, 1, :]
 
         def turn_x(t):
-            c, cols = home[t]
-            t0, nt = CHUNKS[c]
-            if t == t0:
-                xt4[c] = pool.tile([P, G, nt * B, 2], F32, name="xt4", align_bytes=64)
-            bank = ps2.tile([P, G, 2, B], F32, name="bank2")
-            w32 = xraw[t].bitcast(F32)
+            half = t // HALF
+            if t % HALF == 0:
+                x_words[half] = pool.tile([P, G, HALF * B, 2], F32, name="x_words", align_bytes=64)
+            turned_bank[t] = psum_b.tile([P, G, 2, B], F32, name="bank_b")
+            row_words = arrived_x[t].bitcast(F32)
             for g in range(G):
-                for u in range(2):
-                    nc.tensor.transpose(bank[:, g, u, :], w32[:, 256 * g + u : 256 * (g + 1) : 2], ident[:])
-            copy_out(XE[t], xt4[c][:, :, cols, :], bank[:].rearrange("p g u b -> p g b u"))
+                for e in range(2):
+                    nc.tensor.transpose(
+                        turned_bank[t][:, g, e, :], row_words[:, 256 * g + e : 256 * (g + 1) : 2], identity[:]
+                    )
 
-        def xt_bf16(c, g):
-            return xt4[c][:, g, :, :].rearrange("p n u -> p (n u)").bitcast(BF16)
+        def keep_x(t, copy):
+            copy(
+                out=x_words[t // HALF][:, :, in_half(t), :],
+                in_=turned_bank[t][:].rearrange("p g e b -> p g b e"),
+            )
 
-        def quantize_x(c, g, part, parts):
-            t0, nt = CHUNKS[c]
-            if g == 0 and part == 0:
-                xq[c] = pool.tile([P, G, nt * B], I32, name="xq", align_bytes=64)
-                xs[c] = pool.tile([P, G, nt * B], U8, name="xs", align_bytes=64)
-            w = nt * B // parts
-            cols = slice(part * w, (part + 1) * w)
+        def x_lanes(half, g):
+            return x_words[half][:, g, :, :].rearrange("p n e -> p (n e)").bitcast(BF16)
+
+        def quantize_x(t, steps, g):
+            half = t // HALF
+            if g == 0 and t % HALF == 0:
+                x_codes[half] = pool.tile([P, G, HALF * B], I32, name="x_codes", align_bytes=64)
+                x_scales[half] = pool.tile([P, G, HALF * B], U8, name="x_scales", align_bytes=64)
+            cols = in_half(t, steps)
             nc.vector.quantize_mx(
-                out=xq[c][:, g, cols].bitcast(FP8X4), scales=xs[c][:, g, cols],
-                in_=xt_bf16(c, g)[:, part * w * PACK : (part + 1) * w * PACK])
+                out=x_codes[half][:, g, cols].bitcast(FP8X4),
+                scales=x_scales[half][:, g, cols],
+                in_=x_lanes(half, g)[:, LANES * cols.start : LANES * cols.stop],
+            )
 
-        a, u, v, bank_r, bank_i = {}, {}, {}, {}, {}
+        decay, root, state, bank_r, bank_i = {}, {}, {}, {}, {}
 
-        def slots(c):
-            w = 4 // CHUNKS[c][1]
-            return [(g, j0, w) for g in range(G) for j0 in range(0, PACK, w)]
+        def units(half):
+            t = HALF * half
+            if half == 0:
+                lead = [(0, j, 2, t + dt, 2) for dt in (0, 2) for j in (0, 2)]
+            else:
+                lead = [(0, j, 1, t, HALF) for j in range(LANES)]
+            return lead + [(1, j, 1, t, HALF) for j in range(LANES)]
 
-        def gate_matmul(c, g, j0, w):
-            n = CHUNKS[c][1] * B
-            for name, banks in (("r", bank_r), ("i", bank_i)):
-                bank = ps1.tile([P, 512], F32, name="bank1")
-                banks[c, g, j0] = bank
-                for j in range(w):
-                    col = g * GC + (j0 + j) * P
+        def gate_products(unit):
+            g, j0, lanes, t, steps = unit
+            half, cols, width = t // HALF, in_half(t, steps), steps * B
+            for w, banks in (("r", bank_r), ("i", bank_i)):
+                banks[unit] = psum_a.tile([P, BANK], F32, name="bank_a")
+                for n in range(lanes):
                     for k in range(G):
-                        sp, row = plane[name, k]
+                        codes, scale_bytes = weight(w, k, g * GROUP + (j0 + n) * P, P)
                         nc.tensor.matmul_mx(
-                            out=bank[:, j * n : (j + 1) * n],
-                            lhsT=wp[name][:, k, col : col + P].bitcast(FP8X4),
-                            lhsT_scale=sp[row:P, col : col + P],
-                            rhs=xq[c][:, k, :].bitcast(FP8X4),
-                            rhs_scale=xs[c][:, k, :],
+                            out=banks[unit][:, n * width : (n + 1) * width],
+                            lhsT=codes,
+                            lhsT_scale=scale_bytes,
+                            rhs=x_codes[half][:, k, cols].bitcast(FP8X4),
+                            rhs_scale=x_scales[half][:, k, cols],
                             start=(k == 0),
                             stop=(k == G - 1),
                         )
 
-        def flat(t_, j0, w):
-            return t_[:, j0 : j0 + w, :].rearrange("p j n -> p (j n)")
+        def gate_functions(unit):
+            g, j0, lanes, t, steps = unit
+            half, cols, width = t // HALF, in_half(t, steps), steps * B
+            if half not in decay:
+                decay[half] = pool.tile([P, G, LANES, HALF * B], F32, name="decay")
+                state[half] = pool.tile([P, G, LANES, HALF * B], F32, name="state")
+                root[half] = pool.tile([P, G, LANES, HALF * B], F32, name="root")
+            for tile, banks in ((decay[half], bank_r), (state[half], bank_i)):
+                nc.scalar.activation(
+                    out=tile[:, g, j0 : j0 + lanes, cols],
+                    in_=banks[unit][:].rearrange("p (j n) -> p j n", n=width),
+                    func=ACT.Tanh,
+                    scale=0.5,
+                )
+            for j in range(j0, j0 + lanes):
+                alone = cols.start + (B if t == 0 else 0)
+                squares = cols.stop if (half, g, j) in SQUARES_ON_SCALAR else alone
+                if squares > cols.start:
+                    nc.scalar.activation(
+                        out=root[half][:, g, j, cols.start : squares],
+                        in_=decay[half][:, g, j, cols.start : squares],
+                        func=ACT.Exp,
+                        scale=of_channel(log_a_twice, g, j),
+                        bias=of_channel(log_a_twice, g, j),
+                    )
+                nc.scalar.activation(
+                    out=decay[half][:, g, j, alone : cols.stop],
+                    in_=decay[half][:, g, j, alone : cols.stop],
+                    func=ACT.Exp,
+                    scale=of_channel(log_a, g, j),
+                    bias=of_channel(log_a, g, j),
+                )
 
-        def gate_act(c, g, j0, w):
-            n = CHUNKS[c][1] * B
-            if g == 0 and j0 == 0:
-                a[c] = pool.tile([P, G, PACK, n], F32, name="a")
-                u[c] = pool.tile([P, G, PACK, n], F32, name="u")
-                v[c] = pool.tile([P, G, PACK, n], F32, name="v")
-            nc.scalar.activation(out=flat(a[c][:, g], j0, w), in_=bank_r[c, g, j0][:], func=ACT.Tanh, scale=0.5)
-            nc.scalar.activation(out=flat(u[c][:, g], j0, w), in_=bank_i[c, g, j0][:], func=ACT.Tanh, scale=0.5)
-            for j in range(j0, j0 + w):
-                col = slice(g * PACK + j, g * PACK + j + 1)
-                first = FIRST if c == 0 else 0
-                sq = n if g * PACK + j0 in SQ_ACT[c] else first
-                if sq:
-                    nc.scalar.activation(out=v[c][:, g, j, :sq], in_=a[c][:, g, j, :sq], func=ACT.Exp,
-                                         scale=l2[:, col], bias=l2[:, col])
-                nc.scalar.activation(out=a[c][:, g, j, first:], in_=a[c][:, g, j, first:], func=ACT.Exp,
-                                     scale=l1[:, col], bias=l1[:, col])
+        def gate_input(unit):
+            g, j0, lanes, t, steps = unit
+            half, cols = t // HALF, in_half(t, steps)
+            x_by_lane = x_lanes(half, g).rearrange("p (n j) -> p j n", j=LANES)
+            tile = state[half][:, g, j0 : j0 + lanes, cols]
+            nc.vector.scalar_tensor_tensor(
+                out=tile, in0=tile, scalar=1.0, in1=x_by_lane[:, j0 : j0 + lanes, cols], op0=ALU.add, op1=ALU.mult
+            )
 
-        def gate_vec(c, g, j0, w):
-            xb = xt_bf16(c, g).rearrange("p (n j) -> p j n", j=PACK)
-            ug = u[c][:, g, j0 : j0 + w, :]
-            nc.vector.scalar_tensor_tensor(out=ug, in0=ug, scalar=1.0, in1=xb[:, j0 : j0 + w, :], op0=ALU.add, op1=ALU.mult)
+        def square(unit):
+            g, j0, lanes, t, steps = unit
+            half, cols = t // HALF, in_half(t, steps)
+            cols = slice(cols.start + (B if t == 0 else 0), cols.stop)
+            tile = decay[half][:, g, j0 : j0 + lanes, cols]
+            nc.vector.tensor_tensor(out=root[half][:, g, j0 : j0 + lanes, cols], in0=tile, in1=tile, op=ALU.mult)
 
-        def square(c, g, j0, w):
-            first = FIRST if c == 0 else 0
-            ag = a[c][:, g, j0 : j0 + w, first:]
-            nc.vector.tensor_tensor(out=v[c][:, g, j0 : j0 + w, first:], in0=ag, in1=ag, op=ALU.mult)
+        def square_root(half, g):
+            for j in range(0, LANES, 2):
+                tile = root[half][:, g, j : j + 2, :].rearrange("p j n -> p (j n)")
+                nc.scalar.activation(out=tile, in_=tile, func=ACT.Sqrt, scale=-0.25, bias=0.25)
 
-        def root(c, g):
-            for j in range(0, PACK, RP):
-                vv = flat(v[c][:, g], j, RP)
-                nc.scalar.activation(out=vv, in_=vv, func=ACT.Sqrt, scale=-0.25, bias=0.25)
-
-        def drive(c, g, j):
-            col = slice(g * PACK + j, g * PACK + j + 1)
-            nc.vector.scalar_tensor_tensor(out=u[c][:, g, j, :], in0=v[c][:, g, j, :], scalar=gain_f[:, col],
-                                           in1=u[c][:, g, j, :], op0=ALU.mult, op1=ALU.mult)
-
-        tmp = {}
-
-        def recur_mul(t):
-            c, cols = home[t]
-            pc, pcols = home[t - 1]
-            tmp[t] = pool.tile([P, G, PACK, B], F32, name="tmp")
-            nc.vector.tensor_tensor(
-                out=tmp[t][:].rearrange("p g j b -> p (g j) b"), in0=a[c][:].rearrange("p g j n -> p (g j) n")[:, :, cols],
-                in1=u[pc][:].rearrange("p g j n -> p (g j) n")[:, :, pcols], op=ALU.mult)
-
-        def recur_add(t):
-            c, cols = home[t]
-            h = u[c][:].rearrange("p g j n -> p (g j) n")[:, :, cols]
-            nc.vector.tensor_tensor(out=h, in0=h, in1=tmp[t][:].rearrange("p g j b -> p (g j) b"), op=ALU.add)
-
-        hb, hq, hs = {}, {}, {}
-
-        def recur_last(g):
-            t = T - 1
-            c, cols = home[t]
-            if g == 0:
-                hb[t] = pool.tile([P, G, B, PACK], BF16, name="hb", align_bytes=64)
-            nc.vector.tensor_tensor(out=hb[t][:, g].rearrange("p (n i) j -> p n j i", i=4),
-                                    in0=u[c][:, g, :, cols].rearrange("p j (n i) -> p n j i", i=4),
-                                    in1=tmp[t][:, g].rearrange("p j (n i) -> p n j i", i=4), op=ALU.add)
-
-        def cast_h(t):
-            c, cols = home[t]
-            hb[t] = pool.tile([P, G, B, PACK], BF16, name="hb", align_bytes=64)
+        def drive(half):
             for g in range(G):
-                copy_out(CAST[t][g], hb[t][:, g].rearrange("p (n i) j -> p n j i", i=4),
-                         u[c][:, g, :, cols].rearrange("p j (n i) -> p n j i", i=4))
+                for j in range(LANES):
+                    nc.vector.scalar_tensor_tensor(
+                        out=state[half][:, g, j, :],
+                        in0=root[half][:, g, j, :],
+                        scalar=of_channel(gain_f, g, j),
+                        in1=state[half][:, g, j, :],
+                        op0=ALU.mult,
+                        op1=ALU.mult,
+                    )
 
-        def quantize_h(t, split=False):
-            hq[t] = pool.tile([P, G, B], I32, name="hq", bufs=4, align_bytes=64)
-            hs[t] = pool.tile([P, G, B], U8, name="hs", bufs=4, align_bytes=64)
-            for gs in ((slice(0, 1), slice(1, 2)) if split else (slice(0, 2),)):
-                nc.vector.quantize_mx(out=hq[t][:, gs].rearrange("p g n -> p (g n)").bitcast(FP8X4),
-                                      scales=hs[t][:, gs].rearrange("p g n -> p (g n)"),
-                                      in_=hb[t][:, gs].rearrange("p g n j -> p (g n j)"))
+        carried, rounded, h_codes, h_scales = {}, {}, {}, {}
 
-        osb, ob, pq = {}, {}, {}
-        psc = keep.tile([P, G, T, B], U8, name="psc", align_bytes=64)
+        def step_of(tiles, t):
+            return tiles[t // HALF][:].rearrange("p g j n -> p (g j) n")[:, :, in_half(t)]
 
-        def copy_out(engine, dst, src):
-            if engine == "a":
-                nc.scalar.copy(out=dst, in_=src)
-            else:
-                nc.vector.tensor_copy(out=dst, in_=src)
+        def carry(t):
+            carried[t] = pool.tile([P, G, LANES, B], F32, name="carried")
+            nc.vector.tensor_tensor(
+                out=carried[t][:].rearrange("p g j b -> p (g j) b"),
+                in0=step_of(decay, t),
+                in1=step_of(state, t - 1),
+                op=ALU.mult,
+            )
+
+        def add_drive(t):
+            nc.vector.tensor_tensor(
+                out=step_of(state, t),
+                in0=step_of(state, t),
+                in1=carried[t][:].rearrange("p g j b -> p (g j) b"),
+                op=ALU.add,
+            )
+
+        def lanes_side_by_side(t, g):
+            return rounded[t][:, g].rearrange("p (n i) j -> p n j i", i=4)
+
+        def four_neighbours(lanes):
+            return lanes.rearrange("p j (n i) -> p n j i", i=4)
+
+        def round_state(t):
+            rounded[t] = pool.tile([P, G, B, LANES], BF16, name="rounded", align_bytes=64)
+            for g in range(G):
+                nc.vector.tensor_copy(
+                    out=lanes_side_by_side(t, g), in_=four_neighbours(state[t // HALF][:, g, :, in_half(t)])
+                )
+
+        def add_drive_and_round(t):
+            rounded[t] = pool.tile([P, G, B, LANES], BF16, name="rounded", align_bytes=64)
+            for g in range(G):
+                nc.vector.tensor_tensor(
+                    out=lanes_side_by_side(t, g),
+                    in0=four_neighbours(state[t // HALF][:, g, :, in_half(t)]),
+                    in1=four_neighbours(carried[t][:, g]),
+                    op=ALU.add,
+                )
+
+        def quantize_state(t, groups_at_once):
+            h_codes[t] = pool.tile([P, G, B], I32, name="h_codes", bufs=4, align_bytes=64)
+            h_scales[t] = pool.tile([P, G, B], U8, name="h_scales", bufs=4, align_bytes=64)
+            for g in range(0, G, groups_at_once):
+                groups = slice(g, g + groups_at_once)
+                nc.vector.quantize_mx(
+                    out=h_codes[t][:, groups].rearrange("p g n -> p (g n)").bitcast(FP8X4),
+                    scales=h_scales[t][:, groups].rearrange("p g n -> p (g n)"),
+                    in_=rounded[t][:, groups].rearrange("p g n j -> p (g n j)"),
+                )
+
+        out_rows, out_lanes, out_codes = {}, {}, {}
+        out_scales = keep.tile([P, G, T, B], U8, name="out_scales", align_bytes=64)
 
         def project_rows(t, h):
             if h == 0:
-                osb[t] = pool.tile([P, N], F32, name="osb", bufs=3)
-            bank = ps1.tile([P, 512], F32, name="bank1")
+                out_rows[t] = pool.tile([P, N], F32, name="out_rows", bufs=3)
+            bank = psum_a.tile([P, BANK], F32, name="bank_a")
             for k in range(G):
-                sp, row = plane["o", k]
+                codes, scale_bytes = weight("o", k, h * GROUP, GROUP)
                 nc.tensor.matmul_mx(
-                    out=bank[:], lhsT=hq[t][:, k, :].bitcast(FP8X4), lhsT_scale=hs[t][:, k, :],
-                    rhs=wp["o"][:, k, h * GC : (h + 1) * GC].bitcast(FP8X4),
-                    rhs_scale=sp[row:P, h * GC : (h + 1) * GC], start=(k == 0), stop=(k == G - 1))
-            copy_out(OE_ROW[t][h], osb[t][:, h * GC : (h + 1) * GC].rearrange("p (m j) -> p m j", j=PACK),
-                     bank[:].rearrange("p (j m) -> p m j", j=PACK))
+                    out=bank[:],
+                    lhsT=h_codes[t][:, k, :].bitcast(FP8X4),
+                    lhsT_scale=h_scales[t][:, k, :],
+                    rhs=codes,
+                    rhs_scale=scale_bytes,
+                    start=(k == 0),
+                    stop=(k == G - 1),
+                )
+            cols = slice(h * GROUP, (h + 1) * GROUP)
+            nc.scalar.copy(
+                out=out_rows[t][:, cols].rearrange("p (m j) -> p m j", j=LANES),
+                in_=bank[:].rearrange("p (j m) -> p m j", j=LANES),
+            )
             if t == T - 1:
-                nc.sync.dma_start(out=out_0[t][:, h * GC : (h + 1) * GC], in_=osb[t][:, h * GC : (h + 1) * GC])
+                nc.sync.dma_start(out=out_0[t][:, cols], in_=out_rows[t][:, cols])
             elif h == G - 1:
-                nc.sync.dma_start(out=out_0[t], in_=osb[t][:])
+                nc.sync.dma_start(out=out_0[t], in_=out_rows[t][:])
 
-        def project_cols(t, h):
-            bank = ps2.tile([P, PACK, B], F32, name="bank2")
-            for j in range(PACK):
+        def project_columns(t, h, copy):
+            bank = psum_b.tile([P, LANES, B], F32, name="bank_b")
+            for j in range(LANES):
                 for k in range(G):
-                    sp, row = plane["o", k]
-                    col = h * GC + j * P
+                    codes, scale_bytes = weight("o", k, h * GROUP + j * P, P)
                     nc.tensor.matmul_mx(
-                        out=bank[:, j, :], lhsT=wp["o"][:, k, col : col + P].bitcast(FP8X4),
-                        lhsT_scale=sp[row:P, col : col + P],
-                        rhs=hq[t][:, k, :].bitcast(FP8X4), rhs_scale=hs[t][:, k, :], start=(k == 0), stop=(k == G - 1))
+                        out=bank[:, j, :],
+                        lhsT=codes,
+                        lhsT_scale=scale_bytes,
+                        rhs=h_codes[t][:, k, :].bitcast(FP8X4),
+                        rhs_scale=h_scales[t][:, k, :],
+                        start=(k == 0),
+                        stop=(k == G - 1),
+                    )
             if h == 0:
-                ob[t] = pool.tile([P, G, B, PACK], BF16, name="ob", bufs=4, align_bytes=64)
-            copy_out(OE_COL[t][h], ob[t][:, h], bank[:].rearrange("p j n -> p n j"))
-
-        def quantize_out(t):
-            if t % 2 == 0:
-                pq[t] = pool.tile([P, G, 2, B], I32, name="pq", align_bytes=64)
-            dst = pq[t - t % 2]
-            for h in range(G):
-                nc.vector.quantize_mx(out=dst[:, h, t % 2, :].bitcast(FP8X4), scales=psc[:, h, t, :],
-                                      in_=ob[t][:, h].rearrange("p n j -> p (n j)"))
-            if t % 2:
-                nc.sync.dma_start(out=out_1.rearrange("h p m t -> p h (m t)").bitcast(I32)[:, :, (t - 1) * B : (t + 1) * B],
-                                  in_=dst[:].rearrange("p h t b -> p h (t b)"))
-
-        def store_scales(t0, t1, queue):
-            for q in range(4):
-                queue.dma_start(
-                    out=out_2[:, 4 * q : 4 * q + 4, t0 * B : t1 * B].bitcast(I32).rearrange("h r n -> r h n"),
-                    in_=psc[32 * q : 32 * q + 4, :, t0:t1, :].rearrange("r h t n -> r h (t n)").bitcast(I32))
+                out_lanes[t] = pool.tile([P, G, B, LANES], BF16, name="out_lanes", bufs=4, align_bytes=64)
+            copy(out=out_lanes[t][:, h], in_=bank[:].rearrange("p j n -> p n j"))
 
         def project(t):
             for h in range(G):
-                project_cols(t, h)
+                project_columns(t, h, nc.scalar.copy)
             for h in range(G):
                 project_rows(t, h)
 
-        def spread(items, n):
-            return [items[k * len(items) // n : (k + 1) * len(items) // n] for k in range(n)]
+        def quantize_out(t):
+            if t % 2 == 0:
+                out_codes[t // 2] = pool.tile([P, G, 2, B], I32, name="out_codes", bufs=4, align_bytes=64)
+            codes = out_codes[t // 2]
+            for h in range(G):
+                nc.vector.quantize_mx(
+                    out=codes[:, h, t % 2, :].bitcast(FP8X4),
+                    scales=out_scales[:, h, t, :],
+                    in_=out_lanes[t][:, h].rearrange("p n j -> p (n j)"),
+                )
+            if t % 2 == 1:
+                nc.sync.dma_start(
+                    out=out_1.rearrange("h p m t -> p h (m t)").bitcast(I32)[:, :, (t - 1) * B : (t + 1) * B],
+                    in_=codes[:].rearrange("p h t b -> p h (t b)"),
+                )
 
-        def steps(c):
-            return range(CHUNKS[c][0], CHUNKS[c][0] + CHUNKS[c][1])
-
-        def weave(main, extra):
-            done = 0
-            for k, f in enumerate(main):
-                f()
-                while done < len(extra) * (k + 1) // len(main):
-                    extra[done]()
-                    done += 1
+        def store_out_scales(t0, t1):
+            for q in range(P // QUADRANT):
+                nc.sync.dma_start(
+                    out=out_2[:, 4 * q : 4 * q + 4, t0 * B : t1 * B].bitcast(I32).rearrange("h r n -> r h n"),
+                    in_=out_scales[QUADRANT * q : QUADRANT * q + 4, :, t0:t1, :]
+                    .rearrange("r h t n -> r h (t n)")
+                    .bitcast(I32),
+                )
 
         load_x(0)
-        load_scales("r", nc.sync)
-        load_w("r", 0)
+        load_scale_rows("r")
+        load_words("r", 0)
         load_x(2)
-        load_scales("i", nc.sync)
-        load_w("i", 0)
-        load_w("r", 1)
-        load_w("i", 1)
-        softplus_act()
+        load_scale_rows("i")
+        load_words("i", 0)
+        load_words("r", 1)
+        load_words("i", 1)
+        channel_constants_on_scalar()
         turn_x(0)
+        keep_x(0, nc.vector.tensor_copy)
         turn_x(1)
+        keep_x(1, nc.scalar.copy)
         load_x(4)
-        quantize_x(0, 0, 0, 2)
-        quantize_x(0, 1, 0, 2)
-        permute_w("r", 0)
-        permute_s("g", 0)
+        move_words("r", 0)
+        quantize_x(0, 2, 0)
+        quantize_x(0, 2, 1)
+        move_scales("gates", 0)
+        move_words("i", 0)
+
+        first = units(0)
         turn_x(2)
         turn_x(3)
+        gate_products(first[0])
+        channel_constants_on_gpsimd()
+        gate_functions(first[0])
+        keep_x(2, nc.vector.tensor_copy)
+        keep_x(3, nc.vector.tensor_copy)
         load_x(6)
-        quantize_x(0, 0, 1, 2)
-        quantize_x(0, 1, 1, 2)
-        permute_w("i", 0)
-        softplus_vec()
-        load_scales("o", nc.sync)
-        for h in range(G):
-            load_w("o", h)
-        early = [
-            lambda: (permute_w("r", 1), permute_s("g", 1)), lambda: permute_w("i", 1),
-            lambda: (turn_x(4), turn_x(5)), lambda: (turn_x(6), turn_x(7)),
-            lambda: quantize_x(1, 0, 0, 1), lambda: quantize_x(1, 1, 0, 1),
-            lambda: (permute_s("o", 0), permute_s("o", 1)), lambda: permute_w("o", 0)]
-        sl = slots(0)
-        gate_matmul(0, *sl[0])
-        es = spread(early, 8)
-        for k in range(8):
-            gate_act(0, *sl[k])
-            if k < 7:
-                gate_matmul(0, *sl[k + 1])
-            if k % 2:
-                gate_vec(0, sl[k][0], sl[k][1] - 1, 2)
-                if k < 7:
-                    square(0, sl[k][0], sl[k][1] - 1, 2)
-            if k >= 6:
-                square(0, sl[k][0], sl[k][1], 1)
-            for f in es[k]:
-                f()
-        root(0, 0)
-        root(0, 1)
-        sl = slots(1)
-        for s in sl:
-            gate_matmul(1, *s)
-            gate_act(1, *s)
+        quantize_x(2, 2, 0)
+        quantize_x(2, 2, 1)
+        load_scale_rows("o")
+        load_words("o", 0)
+        load_words("o", 1)
 
-        def drive_all(c):
-            for g in range(G):
-                for j in range(PACK):
-                    drive(c, g, j)
+        def turn_and_keep_x(t):
+            for step in (t, t + 1):
+                turn_x(step)
+                keep_x(step, nc.vector.tensor_copy)
 
-        nsq = PACK * G - len(SQ_ACT[1])
-        drive_all(0)
-        permute_w("o", 1)
-        cast_h(0)
-        for t in range(1, 4):
-            recur_mul(t)
-            quantize_h(t - 1)
-            recur_add(t)
-            if t == 1:
-                gate_vec(1, 0, 0, 2)
-            if t == 2:
-                square(1, 0, 0, 2)
-            if t == 3:
-                gate_vec(1, 0, 2, 2)
-            cast_h(t)
-        square(1, 0, 2, 2)
-        quantize_h(3)
-        if nsq > 4:
-            square(1, 1, 0, nsq - 4)
-        gate_vec(1, 1, 0, 4)
-        for t in range(4):
-            if t == ROOTAT[0]:
-                root(1, 0)
-            if t == ROOTAT[1]:
-                root(1, 1)
+        behind = [
+            lambda: (move_words("r", 1), move_scales("gates", 1)),
+            lambda: move_words("i", 1),
+            lambda: turn_and_keep_x(4),
+            lambda: turn_and_keep_x(6),
+            lambda: quantize_x(4, HALF, 0),
+            lambda: quantize_x(4, HALF, 1),
+            lambda: (move_scales("out", 0), move_scales("out", 1)),
+            lambda: move_words("o", 0),
+        ]
+        for n, unit in enumerate(first):
+            if n > 0:
+                gate_functions(unit)
+            if n + 1 < len(first):
+                gate_products(first[n + 1])
+            if unit[0] == 0:
+                gate_input(unit)
+                square(unit)
+            elif unit[1] == 1:
+                gate_input((1, 0, 2, 0, HALF))
+                square((1, 0, 2, 0, HALF))
+            elif unit[1] == 2:
+                square(unit)
+            elif unit[1] == 3:
+                gate_input((1, 2, 2, 0, HALF))
+                square(unit)
+            behind[n]()
+        square_root(0, 0)
+        square_root(0, 1)
+
+        for unit in units(1):
+            gate_products(unit)
+            gate_functions(unit)
+
+        drive(0)
+        move_words("o", 1)
+        round_state(0)
+        between = {
+            1: lambda: gate_input((0, 0, 2, HALF, HALF)),
+            2: lambda: square((0, 0, 2, HALF, HALF)),
+            3: lambda: gate_input((0, 2, 2, HALF, HALF)),
+        }
+        for t in range(1, HALF):
+            carry(t)
+            quantize_state(t - 1, G)
+            add_drive(t)
+            between[t]()
+            round_state(t)
+        square((0, 2, 2, HALF, HALF))
+        quantize_state(HALF - 1, G)
+        square((1, 0, 2, HALF, HALF))
+        gate_input((1, 0, LANES, HALF, HALF))
+        square_root(1, 0)
+        square_root(1, 1)
+        for t in range(HALF):
             project(t)
-        drive_all(1)
-        recur_mul(4)
+
+        drive(1)
+        carry(4)
         quantize_out(0)
-        recur_add(4)
+        add_drive(4)
         quantize_out(1)
-        recur_mul(5)
-        cast_h(4)
-        recur_add(5)
-        quantize_h(4)
-        project(4)
-        quantize_out(2)
-        recur_mul(6)
-        cast_h(5)
-        recur_add(6)
-        quantize_h(5)
-        project(5)
-        quantize_out(3)
-        store_scales(0, 4, nc.sync)
-        recur_mul(7)
-        cast_h(6)
-        quantize_h(6, True)
-        recur_last(0)
-        recur_last(1)
-        quantize_h(7, True)
+        for t in (5, 6):
+            carry(t)
+            round_state(t - 1)
+            add_drive(t)
+            quantize_state(t - 1, G)
+            project(t - 1)
+            quantize_out(t - 3)
+        store_out_scales(0, HALF)
+
+        carry(7)
+        round_state(6)
+        quantize_state(6, 1)
+        add_drive_and_round(7)
+        quantize_state(7, 1)
         quantize_out(4)
         quantize_out(5)
         project(6)
-        project(7)
         quantize_out(6)
+        for h in range(G):
+            project_columns(7, h, nc.vector.tensor_copy)
         quantize_out(7)
-        store_scales(4, 8, nc.sync)
+        store_out_scales(HALF, T)
+        for h in range(G):
+            project_rows(7, h)

from contextlib import ExitStack

import concourse.mybir as mybir
from concourse.masks import make_identity

T, B, D, N = 8, 128, 1024, 1024
FLOPS = 3 * 2 * T * B * D * N

F32 = mybir.dt.float32
BF16 = mybir.dt.bfloat16
I32 = mybir.dt.int32
U8 = mybir.dt.uint8
FP8X4 = mybir.dt.float8_e4m3fn_x4
ACT = mybir.ActivationFunctionType
ALU = mybir.AluOpType

P = 128
LANES = 4
GROUP = P * LANES
G = D // GROUP
HALF = 4
BANK = 512
QUADRANT = 32
SQUARES_ON_SCALAR = ((1, 1, 2), (1, 1, 3))


def tile_rglrueightstepwithoutputprojection_x2_kernel(
    tc, x, wr_words, wr_scales, wi_words, wi_scales, lam, gain, wo_words, wo_scales, out_0, out_1, out_2
):
    nc = tc.nc
    with ExitStack() as ctx:
        keep = ctx.enter_context(tc.tile_pool(name="keep", bufs=1))
        pool = ctx.enter_context(tc.tile_pool(name="pool", bufs=2))
        psum_a = ctx.enter_context(tc.psum_pool(name="psum_a", bufs=4))
        psum_b = ctx.enter_context(tc.psum_pool(name="psum_b", bufs=4))
        ctx.enter_context(tc.manual_schedule())

        arrived_scales = {s: keep.tile([P, D], U8, name="arrived_scales_" + s, align_bytes=64) for s in ("gates", "out")}
        moved_scales = {s: keep.tile([P, D], U8, name="moved_scales_" + s, align_bytes=64) for s in ("gates", "out")}
        moved_words = {w: keep.tile([P, G, D], I32, name="moved_words_" + w, align_bytes=64) for w in ("r", "i", "o")}
        scale_place = {"r": ("gates", 0), "i": ("gates", 8), "o": ("out", 0)}
        words = {"r": wr_words, "i": wi_words, "o": wo_words}
        scales = {"r": wr_scales, "i": wi_scales, "o": wo_scales}

        for s in ("gates", "out"):
            nc.vector.memset(arrived_scales[s][:].bitcast(I32), 0)

        lam_in = keep.tile([P, G, LANES], BF16, name="lam_in")
        gain_in = keep.tile([P, G, LANES], BF16, name="gain_in")
        nc.scalar.dma_start(out=lam_in[:], in_=lam.rearrange("(g p j) -> p g j", g=G, j=LANES))
        nc.gpsimd.dma_start(out=gain_in[:], in_=gain.rearrange("(g p j) -> p g j", g=G, j=LANES))
        identity = keep.tile([P, P], F32, name="identity")
        make_identity(nc, identity[:])

        def load_scale_rows(w):
            s, first_row = scale_place[w]
            for q in range(P // QUADRANT):
                row = QUADRANT * q + first_row
                nc.sync.dma_start(
                    out=arrived_scales[s][row : row + 4 * G, :].bitcast(I32),
                    in_=scales[w][:, 4 * q : 4 * q + 4, :].bitcast(I32),
                )

        arrived_words = {}

        def load_words(w, h):
            arrived_words[w, h] = pool.tile([P, G, GROUP], I32, name="arrived_words", bufs=4)
            nc.sync.dma_start(
                out=arrived_words[w, h][:],
                in_=words[w].rearrange("k p n t -> p k (n t)").bitcast(I32)[:, :, h * GROUP : (h + 1) * GROUP],
            )

        def move_words(w, h):
            nc.vector.tensor_copy(
                out=moved_words[w][:, :, h * GROUP : (h + 1) * GROUP].rearrange("p k (j m) -> p k m j", j=LANES),
                in_=arrived_words[w, h][:].rearrange("p k (m j) -> p k m j", j=LANES),
            )

        def move_scales(s, h):
            cols = slice(h * GROUP, (h + 1) * GROUP)
            nc.vector.tensor_copy(
                out=moved_scales[s][:, cols].rearrange("p (j m) -> p j m", j=LANES),
                in_=arrived_scales[s][:, cols].rearrange("p (m j) -> p j m", j=LANES),
            )

        def weight(w, k, first, width):
            s, first_row = scale_place[w]
            cols = slice(first, first + width)
            return moved_words[w][:, k, cols].bitcast(FP8X4), moved_scales[s][first_row + 4 * k : P, cols]

        log_a = keep.tile([P, G * LANES], F32, name="log_a")
        log_a_twice = keep.tile([P, G * LANES], F32, name="log_a_twice")
        gain_f = keep.tile([P, G * LANES], F32, name="gain_f")
        lam_flat = lam_in[:].rearrange("p g j -> p (g j)")
        log_term = keep.tile([P, G * LANES], F32, name="log_term")
        softplus = keep.tile([P, G * LANES], F32, name="softplus")

        def channel_constants_on_scalar():
            nc.scalar.activation(out=log_term[:], in_=lam_flat, func=ACT.Abs)
            nc.scalar.activation(out=log_term[:], in_=log_term[:], func=ACT.Exp, scale=-1.0)
            nc.scalar.activation(out=log_term[:], in_=log_term[:], func=ACT.Ln, bias=1.0)

        def channel_constants_on_gpsimd():
            nc.gpsimd.tensor_scalar_max(softplus[:], lam_flat, 0.0)
            nc.gpsimd.tensor_tensor(out=softplus[:], in0=softplus[:], in1=log_term[:], op=ALU.add)
            nc.gpsimd.tensor_scalar_mul(log_a[:], softplus[:], -4.0)
            nc.gpsimd.tensor_scalar_mul(log_a_twice[:], softplus[:], -8.0)
            nc.gpsimd.tensor_copy(out=gain_f[:], in_=gain_in[:].rearrange("p g j -> p (g j)"))

        def of_channel(values, g, j):
            return values[:, g * LANES + j : g * LANES + j + 1]

        def in_half(t, steps=1):
            return slice((t % HALF) * B, (t % HALF + steps) * B)

        arrived_x, turned_bank, x_words, x_codes, x_scales = {}, {}, {}, {}, {}

        def load_x(t):
            pair = pool.tile([P, 2, D], BF16, name="arrived_x")
            nc.sync.dma_start(out=pair[:], in_=x[t : t + 2].rearrange("t b d -> b t d"))
            arrived_x[t], arrived_x[t + 1] = pair[:, 0, :], pair[:, 1, :]

        def turn_x(t):
            half = t // HALF
            if t % HALF == 0:
                x_words[half] = pool.tile([P, G, HALF * B, 2], F32, name="x_words", align_bytes=64)
            turned_bank[t] = psum_b.tile([P, G, 2, B], F32, name="bank_b")
            row_words = arrived_x[t].bitcast(F32)
            for g in range(G):
                for e in range(2):
                    nc.tensor.transpose(
                        turned_bank[t][:, g, e, :], row_words[:, 256 * g + e : 256 * (g + 1) : 2], identity[:]
                    )

        def keep_x(t, copy):
            copy(
                out=x_words[t // HALF][:, :, in_half(t), :],
                in_=turned_bank[t][:].rearrange("p g e b -> p g b e"),
            )

        def x_lanes(half, g):
            return x_words[half][:, g, :, :].rearrange("p n e -> p (n e)").bitcast(BF16)

        def quantize_x(t, steps, g):
            half = t // HALF
            if g == 0 and t % HALF == 0:
                x_codes[half] = pool.tile([P, G, HALF * B], I32, name="x_codes", align_bytes=64)
                x_scales[half] = pool.tile([P, G, HALF * B], U8, name="x_scales", align_bytes=64)
            cols = in_half(t, steps)
            nc.vector.quantize_mx(
                out=x_codes[half][:, g, cols].bitcast(FP8X4),
                scales=x_scales[half][:, g, cols],
                in_=x_lanes(half, g)[:, LANES * cols.start : LANES * cols.stop],
            )

        decay, root, state, bank_r, bank_i = {}, {}, {}, {}, {}

        def units(half):
            t = HALF * half
            if half == 0:
                lead = [(0, j, 2, t + dt, 2) for dt in (0, 2) for j in (0, 2)]
            else:
                lead = [(0, j, 1, t, HALF) for j in range(LANES)]
            return lead + [(1, j, 1, t, HALF) for j in range(LANES)]

        def gate_products(unit):
            g, j0, lanes, t, steps = unit
            half, cols, width = t // HALF, in_half(t, steps), steps * B
            for w, banks in (("r", bank_r), ("i", bank_i)):
                banks[unit] = psum_a.tile([P, BANK], F32, name="bank_a")
                for n in range(lanes):
                    for k in range(G):
                        codes, scale_bytes = weight(w, k, g * GROUP + (j0 + n) * P, P)
                        nc.tensor.matmul_mx(
                            out=banks[unit][:, n * width : (n + 1) * width],
                            lhsT=codes,
                            lhsT_scale=scale_bytes,
                            rhs=x_codes[half][:, k, cols].bitcast(FP8X4),
                            rhs_scale=x_scales[half][:, k, cols],
                            start=(k == 0),
                            stop=(k == G - 1),
                        )

        def gate_functions(unit):
            g, j0, lanes, t, steps = unit
            half, cols, width = t // HALF, in_half(t, steps), steps * B
            if half not in decay:
                decay[half] = pool.tile([P, G, LANES, HALF * B], F32, name="decay")
                state[half] = pool.tile([P, G, LANES, HALF * B], F32, name="state")
                root[half] = pool.tile([P, G, LANES, HALF * B], F32, name="root")
            for tile, banks in ((decay[half], bank_r), (state[half], bank_i)):
                nc.scalar.activation(
                    out=tile[:, g, j0 : j0 + lanes, cols],
                    in_=banks[unit][:].rearrange("p (j n) -> p j n", n=width),
                    func=ACT.Tanh,
                    scale=0.5,
                )
            for j in range(j0, j0 + lanes):
                alone = cols.start + (B if t == 0 else 0)
                squares = cols.stop if (half, g, j) in SQUARES_ON_SCALAR else alone
                if squares > cols.start:
                    nc.scalar.activation(
                        out=root[half][:, g, j, cols.start : squares],
                        in_=decay[half][:, g, j, cols.start : squares],
                        func=ACT.Exp,
                        scale=of_channel(log_a_twice, g, j),
                        bias=of_channel(log_a_twice, g, j),
                    )
                nc.scalar.activation(
                    out=decay[half][:, g, j, alone : cols.stop],
                    in_=decay[half][:, g, j, alone : cols.stop],
                    func=ACT.Exp,
                    scale=of_channel(log_a, g, j),
                    bias=of_channel(log_a, g, j),
                )

        def gate_input(unit):
            g, j0, lanes, t, steps = unit
            half, cols = t // HALF, in_half(t, steps)
            x_by_lane = x_lanes(half, g).rearrange("p (n j) -> p j n", j=LANES)
            tile = state[half][:, g, j0 : j0 + lanes, cols]
            nc.vector.scalar_tensor_tensor(
                out=tile, in0=tile, scalar=1.0, in1=x_by_lane[:, j0 : j0 + lanes, cols], op0=ALU.add, op1=ALU.mult
            )

        def square(unit):
            g, j0, lanes, t, steps = unit
            half, cols = t // HALF, in_half(t, steps)
            cols = slice(cols.start + (B if t == 0 else 0), cols.stop)
            tile = decay[half][:, g, j0 : j0 + lanes, cols]
            nc.vector.tensor_tensor(out=root[half][:, g, j0 : j0 + lanes, cols], in0=tile, in1=tile, op=ALU.mult)

        def square_root(half, g):
            for j in range(0, LANES, 2):
                tile = root[half][:, g, j : j + 2, :].rearrange("p j n -> p (j n)")
                nc.scalar.activation(out=tile, in_=tile, func=ACT.Sqrt, scale=-0.25, bias=0.25)

        def drive(half):
            for g in range(G):
                for j in range(LANES):
                    nc.vector.scalar_tensor_tensor(
                        out=state[half][:, g, j, :],
                        in0=root[half][:, g, j, :],
                        scalar=of_channel(gain_f, g, j),
                        in1=state[half][:, g, j, :],
                        op0=ALU.mult,
                        op1=ALU.mult,
                    )

        carried, rounded, h_codes, h_scales = {}, {}, {}, {}

        def step_of(tiles, t):
            return tiles[t // HALF][:].rearrange("p g j n -> p (g j) n")[:, :, in_half(t)]

        def carry(t):
            carried[t] = pool.tile([P, G, LANES, B], F32, name="carried")
            nc.vector.tensor_tensor(
                out=carried[t][:].rearrange("p g j b -> p (g j) b"),
                in0=step_of(decay, t),
                in1=step_of(state, t - 1),
                op=ALU.mult,
            )

        def add_drive(t):
            nc.vector.tensor_tensor(
                out=step_of(state, t),
                in0=step_of(state, t),
                in1=carried[t][:].rearrange("p g j b -> p (g j) b"),
                op=ALU.add,
            )

        def lanes_side_by_side(t, g):
            return rounded[t][:, g].rearrange("p (n i) j -> p n j i", i=4)

        def four_neighbours(lanes):
            return lanes.rearrange("p j (n i) -> p n j i", i=4)

        def round_state(t):
            rounded[t] = pool.tile([P, G, B, LANES], BF16, name="rounded", align_bytes=64)
            for g in range(G):
                nc.vector.tensor_copy(
                    out=lanes_side_by_side(t, g), in_=four_neighbours(state[t // HALF][:, g, :, in_half(t)])
                )

        def add_drive_and_round(t):
            rounded[t] = pool.tile([P, G, B, LANES], BF16, name="rounded", align_bytes=64)
            for g in range(G):
                nc.vector.tensor_tensor(
                    out=lanes_side_by_side(t, g),
                    in0=four_neighbours(state[t // HALF][:, g, :, in_half(t)]),
                    in1=four_neighbours(carried[t][:, g]),
                    op=ALU.add,
                )

        def quantize_state(t, groups_at_once):
            h_codes[t] = pool.tile([P, G, B], I32, name="h_codes", bufs=4, align_bytes=64)
            h_scales[t] = pool.tile([P, G, B], U8, name="h_scales", bufs=4, align_bytes=64)
            for g in range(0, G, groups_at_once):
                groups = slice(g, g + groups_at_once)
                nc.vector.quantize_mx(
                    out=h_codes[t][:, groups].rearrange("p g n -> p (g n)").bitcast(FP8X4),
                    scales=h_scales[t][:, groups].rearrange("p g n -> p (g n)"),
                    in_=rounded[t][:, groups].rearrange("p g n j -> p (g n j)"),
                )

        out_rows, out_lanes, out_codes = {}, {}, {}
        out_scales = keep.tile([P, G, T, B], U8, name="out_scales", align_bytes=64)

        def project_rows(t, h):
            if h == 0:
                out_rows[t] = pool.tile([P, N], F32, name="out_rows", bufs=3)
            bank = psum_a.tile([P, BANK], F32, name="bank_a")
            for k in range(G):
                codes, scale_bytes = weight("o", k, h * GROUP, GROUP)
                nc.tensor.matmul_mx(
                    out=bank[:],
                    lhsT=h_codes[t][:, k, :].bitcast(FP8X4),
                    lhsT_scale=h_scales[t][:, k, :],
                    rhs=codes,
                    rhs_scale=scale_bytes,
                    start=(k == 0),
                    stop=(k == G - 1),
                )
            cols = slice(h * GROUP, (h + 1) * GROUP)
            nc.scalar.copy(
                out=out_rows[t][:, cols].rearrange("p (m j) -> p m j", j=LANES),
                in_=bank[:].rearrange("p (j m) -> p m j", j=LANES),
            )
            if t == T - 1:
                nc.sync.dma_start(out=out_0[t][:, cols], in_=out_rows[t][:, cols])
            elif h == G - 1:
                nc.sync.dma_start(out=out_0[t], in_=out_rows[t][:])

        def project_columns(t, h, copy):
            bank = psum_b.tile([P, LANES, B], F32, name="bank_b")
            for j in range(LANES):
                for k in range(G):
                    codes, scale_bytes = weight("o", k, h * GROUP + j * P, P)
                    nc.tensor.matmul_mx(
                        out=bank[:, j, :],
                        lhsT=codes,
                        lhsT_scale=scale_bytes,
                        rhs=h_codes[t][:, k, :].bitcast(FP8X4),
                        rhs_scale=h_scales[t][:, k, :],
                        start=(k == 0),
                        stop=(k == G - 1),
                    )
            if h == 0:
                out_lanes[t] = pool.tile([P, G, B, LANES], BF16, name="out_lanes", bufs=4, align_bytes=64)
            copy(out=out_lanes[t][:, h], in_=bank[:].rearrange("p j n -> p n j"))

        def project(t):
            for h in range(G):
                project_columns(t, h, nc.scalar.copy)
            for h in range(G):
                project_rows(t, h)

        def quantize_out(t):
            if t % 2 == 0:
                out_codes[t // 2] = pool.tile([P, G, 2, B], I32, name="out_codes", bufs=4, align_bytes=64)
            codes = out_codes[t // 2]
            for h in range(G):
                nc.vector.quantize_mx(
                    out=codes[:, h, t % 2, :].bitcast(FP8X4),
                    scales=out_scales[:, h, t, :],
                    in_=out_lanes[t][:, h].rearrange("p n j -> p (n j)"),
                )
            if t % 2 == 1:
                nc.sync.dma_start(
                    out=out_1.rearrange("h p m t -> p h (m t)").bitcast(I32)[:, :, (t - 1) * B : (t + 1) * B],
                    in_=codes[:].rearrange("p h t b -> p h (t b)"),
                )

        def store_out_scales(t0, t1):
            for q in range(P // QUADRANT):
                nc.sync.dma_start(
                    out=out_2[:, 4 * q : 4 * q + 4, t0 * B : t1 * B].bitcast(I32).rearrange("h r n -> r h n"),
                    in_=out_scales[QUADRANT * q : QUADRANT * q + 4, :, t0:t1, :]
                    .rearrange("r h t n -> r h (t n)")
                    .bitcast(I32),
                )

        load_x(0)
        load_scale_rows("r")
        load_words("r", 0)
        load_x(2)
        load_scale_rows("i")
        load_words("i", 0)
        load_words("r", 1)
        load_words("i", 1)
        channel_constants_on_scalar()
        turn_x(0)
        keep_x(0, nc.vector.tensor_copy)
        turn_x(1)
        keep_x(1, nc.scalar.copy)
        load_x(4)
        move_words("r", 0)
        quantize_x(0, 2, 0)
        quantize_x(0, 2, 1)
        move_scales("gates", 0)
        move_words("i", 0)

        first = units(0)
        turn_x(2)
        turn_x(3)
        gate_products(first[0])
        channel_constants_on_gpsimd()
        gate_functions(first[0])
        keep_x(2, nc.vector.tensor_copy)
        keep_x(3, nc.vector.tensor_copy)
        load_x(6)
        quantize_x(2, 2, 0)
        quantize_x(2, 2, 1)
        load_scale_rows("o")
        load_words("o", 0)
        load_words("o", 1)

        def turn_and_keep_x(t):
            for step in (t, t + 1):
                turn_x(step)
                keep_x(step, nc.vector.tensor_copy)

        behind = [
            lambda: (move_words("r", 1), move_scales("gates", 1)),
            lambda: move_words("i", 1),
            lambda: turn_and_keep_x(4),
            lambda: turn_and_keep_x(6),
            lambda: quantize_x(4, HALF, 0),
            lambda: quantize_x(4, HALF, 1),
            lambda: (move_scales("out", 0), move_scales("out", 1)),
            lambda: move_words("o", 0),
        ]
        for n, unit in enumerate(first):
            if n > 0:
                gate_functions(unit)
            if n + 1 < len(first):
                gate_products(first[n + 1])
            if unit[0] == 0:
                gate_input(unit)
                square(unit)
            elif unit[1] == 1:
                gate_input((1, 0, 2, 0, HALF))
                square((1, 0, 2, 0, HALF))
            elif unit[1] == 2:
                square(unit)
            elif unit[1] == 3:
                gate_input((1, 2, 2, 0, HALF))
                square(unit)
            behind[n]()
        square_root(0, 0)
        square_root(0, 1)

        for unit in units(1):
            gate_products(unit)
            gate_functions(unit)

        drive(0)
        move_words("o", 1)
        round_state(0)
        between = {
            1: lambda: gate_input((0, 0, 2, HALF, HALF)),
            2: lambda: square((0, 0, 2, HALF, HALF)),
            3: lambda: gate_input((0, 2, 2, HALF, HALF)),
        }
        for t in range(1, HALF):
            carry(t)
            quantize_state(t - 1, G)
            add_drive(t)
            between[t]()
            round_state(t)
        square((0, 2, 2, HALF, HALF))
        quantize_state(HALF - 1, G)
        square((1, 0, 2, HALF, HALF))
        gate_input((1, 0, LANES, HALF, HALF))
        square_root(1, 0)
        square_root(1, 1)
        for t in range(HALF):
            project(t)

        drive(1)
        carry(4)
        quantize_out(0)
        add_drive(4)
        quantize_out(1)
        for t in (5, 6):
            carry(t)
            round_state(t - 1)
            add_drive(t)
            quantize_state(t - 1, G)
            project(t - 1)
            quantize_out(t - 3)
        store_out_scales(0, HALF)

        carry(7)
        round_state(6)
        quantize_state(6, 1)
        add_drive_and_round(7)
        quantize_state(7, 1)
        quantize_out(4)
        quantize_out(5)
        project(6)
        quantize_out(6)
        for h in range(G):
            project_columns(7, h, nc.vector.tensor_copy)
        quantize_out(7)
        store_out_scales(HALF, T)
        for h in range(G):
            project_rows(7, h)
